import numpy as np, ml_dtypes
CORES = [3,7,11,15,131,135,139,143]
N = 8
import mx_ref
BF = ml_dtypes.bfloat16
def cols(t, e):
    v = np.concatenate([t.reshape(128, -1, 4), np.zeros((128, 1, 4), BF)], axis=1)
    return np.ascontiguousarray(v[:, e]).reshape(128, -1)
def cut(t, i, w=512):
    return t[:, w * i:w * i + w]
def f(rng, *shape):
    return mx_ref.flush((rng.standard_normal(shape, dtype=np.float32) * np.exp2(rng.integers(-2, 3, shape[:-1] + (1,)))).astype(BF))
def wide(rng, *shape, cols=0):
    v = rng.standard_normal(shape, dtype=np.float32) * np.exp2(rng.integers(-12, 13, shape)).astype(np.float32)
    if cols: v *= np.repeat(np.exp2(rng.integers(-cols, cols + 1, shape[:-2] + (1, shape[-1] // 4))) * (rng.random(shape[:-2] + (1, shape[-1] // 4)) > 0.0625), 4, axis=-1).astype(np.float32)
    return mx_ref.flush(v.astype(BF))
P, K, R, O = 128, 32, 5, 2
PART = [1, 2, 4, 1, 2]
def scores(c, qt):
    k = mx_ref.quantize(np.concatenate([qt[r][:, :4 * R] for r in range(N)], axis=1))
    s = [mx_ref.matmul(mx_ref.quantize(cut(c[q], i)), k) for q in range(N) for i in range(P // 128)]
    return np.concatenate(s).reshape(N * P, N, R)
def play(s):
    held, use, out = np.arange(N * P).reshape(N, P), np.zeros((N, P), np.float32), []
    for t in range(R):
        left = []
        for r in range(N):
            v = s[held[r], r, t]
            use[r] = use[r] + v * v
            left.append(np.argsort(use[r], kind="stable")[:K])
        new = held.copy()
        for r in range(N):
            p = r ^ PART[t]
            new[r, left[r]] = held[p, left[p]]
            use[r, left[r]] = 0
        held = new
        out.append(held)
    return np.stack(out)
def fit(s):
    a = np.abs(s)
    return bool(np.isfinite(a).all() and ((a == 0) | (a >= 2.0 ** -60) & (a <= 2.0 ** 60)).all())
def times(t, v):
    return mx_ref.flush((t.astype(np.float32) * np.asarray(v, np.float32)).astype(BF))
def plain(rng):
    q = np.array(f(rng, N, 128, 512))
    q[:, :, 4 * R:] = 0
    return {"c": f(rng, N, 128, 4 * P), "qt": q, "w": f(rng, N, 128, 512 * O)}
def first(make, good=None):
    for i in range(50):
        d = make()
        s = scores(d["c"], d["qt"])
        if fit(s) and (good is None or good(s)): return d
    raise RuntimeError("no draw of 50 is fit")
def athome(s):
    h, a = play(s), np.ones((N, R + 1, P), bool)
    for r in range(N):
        for t in range(R): a[r, t + 1] = np.isin(np.arange(P * r, P * r + P), h[t, r])
    return a
def setup_inputs(rng):
    return first(lambda: plain(rng))
def setup_inputs_sides(rng):
    top = np.arange(128) < 64
    def make():
        d = plain(rng)
        half = np.stack([rng.permutation(P) < P // 2 for r in range(N)])
        d["c"] = times(d["c"], np.repeat(half[:, None, :] == top[None, :, None], 4, axis=2))
        for t in range(R):
            g = np.where(top == (PART[t] == 1), 1.0, 2.0 ** -6) * 4.0 ** t
            d["qt"][:, :, 4 * t:4 * t + 4] = times(d["qt"][:, :, 4 * t:4 * t + 4], g[None, :, None])
        return d
    def good(s):
        a = athome(s)
        return bool((~a[:, :-1] & a[:, 1:]).any(axis=(1, 2)).all())
    return first(make, good)
def setup_inputs_ties(rng):
    def make():
        d = plain(rng)
        d["c"] = np.stack([times(cols(d["c"][r], rng.integers(0, 6, P)), np.repeat(1 - 2 * rng.integers(0, 2, P), 4)) for r in range(N)])
        return d
    def good(s):
        for r in range(N):
            v = s[P * r:P * r + P, r, 0]
            u = np.sort(v * v)
            if u[K - 1] != u[K]: return False
        return True
    return first(make, good)
def setup_inputs_shrink(rng):
    low = np.arange(N) >= N - N // 4
    def make():
        d = plain(rng)
        size = np.exp2(np.where(low, -30.0, 23.0)[:, None] + 2 * rng.random((N, P))) * (1 - 2 * rng.integers(0, 2, (N, P)))
        d["c"] = ((1 + rng.random((N, 128, 4 * P))) * np.repeat(size, 4, axis=1)[:, None, :]).astype(np.float32).astype(BF)
        on = ~low[:, None] | np.stack([rng.permutation(128) < 2 for r in range(N)])
        for t in range(R):
            g = np.exp2(np.where(low, 8.0 * (R - 1 - t) - 30.0, 21.0 - 8.0 * t))
            d["qt"][:, :, 4 * t:4 * t + 4] = ((1 + rng.random((N, 128, 4))) * (g[:, None] * on)[:, :, None]).astype(np.float32).astype(BF)
        return d
    def good(s):
        h, a, b = play(s), np.zeros(N, bool), np.zeros(N, bool)
        for r in range(N):
            at, use, since = np.arange(P * r, P * r + P), np.zeros(P, np.float32), np.zeros(P, int)
            if low[r] and np.abs(s[at, r, R - 1]).max() > 2.0 ** -50 or not low[r] and np.abs(s[at, r, 0]).min() < 2.0 ** 50: return False
            for t in range(R):
                v = s[at, r]
                use = use + v[:, t] * v[:, t]
                sums = np.concatenate([np.zeros((P, 1), np.float32), np.cumsum(v * v, axis=1)], axis=1)
                diff = sums[:, t + 1] - sums[np.arange(P), since]
                a[r] |= (np.argsort(use, kind="stable")[:K] != np.argsort(diff, kind="stable")[:K]).any()
                b[r] |= np.sort(use)[K - 1] > 1e30
                moved = h[t, r] != at
                at = h[t, r]
                use[moved] = 0
                since[moved] = t + 1
        return bool(2 * a.sum() > N and 2 * b.sum() > N)
    return first(make, good)
def setup_inputs_turn(rng):
    on = (np.arange(128) // (128 // N))[None, :] == np.arange(N)[:, None]
    def make():
        d = plain(rng)
        d["c"] = times(d["c"], np.where(on, 2.0 ** -8, 1.0)[:, :, None])
        d["qt"] = times(d["qt"], on[:, :, None])
        return d
    return first(make, lambda s: bool((~athome(s)).any(axis=1).all()))
def setup_inputs_spread(rng):
    return first(lambda: {**plain(rng), "c": wide(rng, N, 128, 4 * P, cols=6)})
def check_inputs(d):
    b = []
    for k in ("c", "qt", "w"):
        v = np.abs(d[k].astype(np.float32))
        if not (np.isfinite(v).all() and ((v == 0) | (v >= 2.0 ** -30) & (v <= 2.0 ** 30)).all()): b.append("a value of " + k)
    if (d["qt"][:, :, 4 * R:].astype(np.float32) != 0).any(): b.append("qt has numbers behind its first R columns")
    if not b and not fit(scores(d["c"], d["qt"])): b.append("a score")
    return b
def reference(c, qt, w):
    held = play(scores(c, qt))
    every = np.concatenate([c[q] for q in range(N)], axis=1)
    y = np.zeros((N, 128, R * O * P), np.float32)
    for r in range(N):
        u, at = np.unique(held[:, r].reshape(-1), return_inverse=True)
        at = at.reshape(R, P)
        q = mx_ref.quantize(cols(every, np.concatenate([u, np.full(-len(u) % 4, -1)])))
        for o in range(O):
            z = mx_ref.matmul(mx_ref.quantize(cut(w[r], o)), q)
            for t in range(R):
                i = (t * O + o) * P
                y[r, :, i:i + P] = z[:, at[t]]
    return {"y": y}

@@ -1,0 +1,468 @@
+from concourse.bass import DstId, RemoteDMATransfer
+from concourse.mybir import dt, AluOpType, AxisListType, ActivationFunctionType
+
+P, K, R, O = 128, 32, 5, 2
+PREV = 1.0 - 2.0 ** -24
+TINY = 2.0 ** -121
+
+F4, BF, U16, CODE, PLANE = "float32", "bfloat16", "uint16", "float8_e4m3fn_x4", "uint8"
+WW = [128, 160, 192, 224, 256, 160]
+
+
+def sb(kind, **widths):
+    return {n: ("sbuf", [128] + (w if isinstance(w, list) else [w]), kind) for n, w in widths.items()}
+
+
+SCRATCH = {"ps": ("psum", [128, 4096], F4)}
+SCRATCH.update(sb(BF, cb=512, qb=20, wb=1024, rb=2560, ptb=128, ones=128, zeros=128, rmc=96, cnt=4,
+                  cm0=512, cm1=512, cs0=512, cs1=512, gj=128, rv=128, vc=128, hb=[2, 128], ht=[2, 128], gm=96,
+                  hc=[2, 64], hd=[2, 64], hp=[2, 64], hq=[2, 64]))
+SCRATCH.update(sb(F4, qrow=128, q32=128, pt=128, pts=128, slr=128, fd=128, j3=[2, 32], js=[2, 32],
+                  sq=640, kk=640, sv=128, km0=128, kt0=128, kd0=128, k40=4, km1=128, kt1=128, kd1=128, k41=4,
+                  lf=4, tf=128, tm=128, tx=32, pb=32, pbc=32, pa=32, pac=32, fa=32, xm=64, svb=32, svc=32,
+                  af=800, asum=32, xa=32, at=32, gs=96, zl=256, zf=64, yy=1536))
+SCRATCH.update(sb(U16, lbu=10, plu=10, lpu=10))
+SCRATCH.update(sb(CODE, rq=640, wq=256))
+SCRATCH.update(sb(PLANE, rs=640, ws=256))
+for _t in range(6):
+    _w = WW[_t] + (96 if _t else 0)
+    SCRATCH.update(sb(CODE, **{"win%d" % _t: _w}))
+    SCRATCH.update(sb(PLANE, **{"wis%d" % _t: _w}))
+for _t in range(5):
+    SCRATCH.update(sb(CODE, **{"out%d" % _t: 32}))
+    SCRATCH.update(sb(PLANE, **{"ous%d" % _t: 128}))
+DSEM = ["dc", "dq", "dw", "do"] + ["dn%d" % t for t in range(1, 6)] + ["dg%d" % t for t in range(2, 5)] + ["dy%d" % t for t in range(6)]
+SEMAPHORES = ["cv", "ca", "ct", "cg"] + DSEM + ["arr%d" % t for t in range(5)] + ["snd%d" % t for t in range(5)]
+
+
+def rank_program(g, core, T, topo):
+    rank = T.rank_of(core)
+    if rank is None:
+        return
+    A, F = AluOpType, ActivationFunctionType
+    eng = {"v": g.vector, "a": g.scalar, "t": g.tensor, "g": g, "s": g.sync}
+    csem = {"v": "cv", "a": "ca", "t": "ct", "g": "cg"}
+    count = {"v": 0, "a": 0, "t": 0, "g": 0}
+    known = {q: {} for q in eng}
+    snap = {}
+    wr, rd = {}, {}
+    ends = {}
+
+    def wait(q, sem, val):
+        if known[q].get(sem, 0) >= val:
+            return
+        eng[q].wait_ge(T.sem[sem], val)
+        known[q][sem] = val
+        for s, v in snap.get((sem, val), {}).items():
+            if known[q].get(s, 0) < v:
+                known[q][s] = v
+
+    def waits(q, reads, writes):
+        need = {}
+        for (n, lo, hi) in reads:
+            for (l, h, q2, s, v) in wr.get(n, ()):
+                if l < hi and lo < h:
+                    need[s] = max(need.get(s, 0), v)
+        for (n, lo, hi) in writes:
+            for (l, h, q2, s, v) in wr.get(n, ()):
+                if l < hi and lo < h:
+                    need[s] = max(need.get(s, 0), v)
+            for (l, h, q2, s, v) in rd.get(n, ()):
+                if l < hi and lo < h and (q2 != q or s[0] == "d"):
+                    need[s] = max(need.get(s, 0), v)
+        for s in sorted(need):
+            wait(q, s, need[s])
+
+    def note(q, reads, writes, sem, val):
+        snap[(sem, val)] = dict(known[q])
+        for (n, lo, hi) in writes:
+            wr[n] = [e for e in wr.get(n, ()) if not (lo <= e[0] and e[1] <= hi)] + [(lo, hi, q, sem, val)]
+            rd[n] = [e for e in rd.get(n, ()) if not (lo <= e[0] and e[1] <= hi)]
+        for (n, lo, hi) in reads:
+            rd.setdefault(n, []).append((lo, hi, q, sem, val))
+
+    def op(q, fn, reads, writes):
+        waits(q, reads, writes)
+        ins = fn()
+        count[q] += 1
+        ins.then_inc(T.sem[csem[q]], 1)
+        note(q, reads, writes, csem[q], count[q])
+
+    def dma(q, sem, *moves):
+        for (out, in_, reads, writes) in moves:
+            waits(q, reads, writes)
+            eng[q].dma_start(out, in_).then_inc(T.sem[sem], 16)
+        ends[sem] = 16 * len(moves)
+        for (out, in_, reads, writes) in moves:
+            note(q, reads, writes, sem, ends[sem])
+
+    def V(n, a, b, step=1):
+        return (T[n][:, a:b] if step == 1 else T[n][:, a:b:step], [(n, a, b)])
+
+    def V3(n, a, b):
+        return (T[n][:, :, a:b], [(n + "0", a, b), (n + "1", a, b)])
+
+    def H(n, j, a, b):
+        return (T[n][:, j, a:b], [(n + str(j), a, b)])
+
+    def IX(v, off):
+        return (v[0].indirect(off[0]), v[1] + off[1])
+
+    def C32(v):
+        return (v[0].bitcast(dt.uint32), v[1])
+
+    def ap(x):
+        return x[0] if isinstance(x, tuple) else x
+
+    def rg(*xs):
+        r = []
+        for x in xs:
+            if isinstance(x, tuple):
+                r += x[1]
+        return r
+
+    def ts(out, i0, s1, op0, s2=None, op1=None):
+        if op1 is None:
+            op("v", lambda: g.vector.tensor_scalar(ap(out), ap(i0), ap(s1), None, op0), rg(i0, s1), rg(out))
+        else:
+            op("v", lambda: g.vector.tensor_scalar(ap(out), ap(i0), ap(s1), ap(s2), op0, op1), rg(i0, s1, s2), rg(out))
+
+    def tt(out, i0, i1, o):
+        op("v", lambda: g.vector.tensor_tensor(ap(out), ap(i0), ap(i1), o), rg(i0, i1), rg(out))
+
+    def cp(out, in_):
+        op("v", lambda: g.vector.tensor_copy(ap(out), ap(in_)), rg(in_), rg(out))
+
+    def scatter(win, off, vals):
+        op("v", lambda: g.vector.tensor_copy(win[0].indirect(off[0]), ap(vals)), rg(off, vals), rg(win))
+
+    def tr(out, in_):
+        op("v", lambda: g.vector.transpose(ap(out), ap(in_)), rg(in_), rg(out))
+
+    def most(out, in_):
+        op("v", lambda: g.vector.tensor_reduce(ap(out), ap(in_), AxisListType.X, A.max), rg(in_), rg(out))
+
+    def scan(out, d0, d1, start=0.0, o=A.add):
+        op("v", lambda: g.vector.tensor_tensor_scan(ap(out), ap(d0), ap(d1), ap(start), A.mult, o), rg(d0, d1, start), rg(out))
+
+    def fill(v, c):
+        op("v", lambda: g.vector.memset(ap(v), c), [], rg(v))
+
+    def quant(q, s, a, b, in_):
+        x, y = V(q, a, b), V(s, a, b)
+        op("v", lambda: g.vector.quantize_mx(x[0], y[0], ap(in_)), rg(in_), rg(x, y))
+
+    def act(out, in_, f, **kw):
+        more = [kw["accum_out"]] if "accum_out" in kw else []
+        op("a", lambda: g.scalar.activation(ap(out), ap(in_), f, **{k: ap(kw[k]) for k in kw}),
+           rg(in_, *[kw[k] for k in kw if k != "accum_out"]), rg(out, *more))
+
+    bank = [0]
+
+    def mm(lq, ls, la, rq, rs, ra):
+        b = 512 * (bank[0] % 8)
+        bank[0] += 1
+        l, m, r, s = V(lq, la, la + 128), V(ls, la, la + 128), V(rq, ra, ra + 128), V(rs, ra, ra + 128)
+        op("t", lambda: g.tensor.matmul_mx(T.ps[:, b:b + 128], l[0], m[0], r[0], s[0], True, True), rg(l, m, r, s), [("ps", b, b + 512)])
+        return b
+
+    def PS(b, lo, hi):
+        return (T.ps[:, b + lo:b + hi], [("ps", b, b + 512)])
+
+    def iota(v, pattern):
+        op("g", lambda: g.iota(v[0], pattern, 0, 0, allow_small_or_imprecise_dtypes=True), [], v[1])
+
+    fillers = []
+
+    def later(f, *args):
+        fillers.append(lambda: f(*args))
+
+    def gap(k=1):
+        for _ in range(k):
+            if fillers:
+                fillers.pop(0)()
+
+    dma("a", "dq", (T.qb[:, 0:20], T.qt[:, 0:20], [], [("qb", 0, 20)]))
+    dma("s", "dc", (T.cb[:, 0:512], T.c[:, 0:512], [], [("cb", 0, 512)]))
+    dma("s", "dw", (T.wb[:, 0:1024], T.w[:, 0:1024], [], [("wb", 0, 1024)]))
+    iota(V("qrow", 0, 128), [[1, 128]])
+    iota(V("q32", 0, 128), [[0, 4], [1, 32]])
+    J3, JS = (T.j3[:, :, :], [("j3", 0, 32)]), (T.js[:, :, :], [("js", 0, 32)])
+    iota(J3, [[16, 2], [0, 2], [1, 16]])
+    fill(V("zeros", 0, 128), 0.0)
+    fill(V("ones", 0, 128), 1.0)
+    fill(V("rmc", 0, 96), 1.0)
+    tr(V("pt", 0, 128), V("qrow", 0, 128))
+    ts(V("fd", 0, 128), V("q32", 0, 128), V("pt", 0, 1), A.is_ge, PREV, A.max)
+    cp(V("ptb", 0, 128), V("pt", 0, 128))
+
+    def rep(t, e, on):
+        o, q = (T.rb[:, 512 * t + e:512 * t + 512:4], [("rb%d" % e, t, t + 1)]), V("qb", 4 * t + e, 4 * t + e + 1)
+        if on == "v":
+            ts(o, V("ones", 0, 128), q, A.mult)
+        else:
+            act(o, V("zeros", 0, 128), F.Identity, bias=q)
+
+    def RB(t, u):
+        return (T.rb[:, 512 * t:512 * u], [("rb%d" % e, t, u) for e in range(4)])
+
+    def square(dst, b, lo, hi):
+        act(dst, PS(b, lo, hi), F.Square)
+
+    def move(m, n, a, b):
+        x, y, s, r = V("win%d" % n, a, b), V("win%d" % m, a, b), V("wis%d" % n, a, b), V("wis%d" % m, a, b)
+        return ((x[0].bitcast(dt.uint8), y[0].bitcast(dt.uint8), y[1], x[1]), (s[0], r[0], r[1], s[1]))
+
+    def SQ(t):
+        return V("sq", 128 * t, 128 * t + 128)
+
+    def KK(t):
+        return V("kk", 128 * t, 128 * t + 128)
+
+    def LB(t):
+        return V("lbu", 2 * t, 2 * t + 2)
+
+    def LP(t):
+        return V("lpu" if t else "lbu", 2 * t, 2 * t + 2)
+
+    def compare(t, k):
+        x = str(t % 2)
+        kn, kl = k[1][0][0], k[1][0][1]
+
+        def turn():
+            tr(V("kt" + x, 0, 128), k)
+            ts(V("km" + x, 0, 128), k, TINY, A.max)
+
+        def second():
+            tt(V("kd" + x, 0, 128), V("km" + x, 0, 128), V("fd", 0, 128), A.mult)
+            ts(V("k4" + x, 0, 4), V("kt" + x, 0, 128, 32), TINY, A.max)
+
+        def run(m):
+            u, c, d = V("kt" + x, 32 * m, 32 * m + 1), 128 * m, 32 * m
+            if m > 0:
+                ts(V("cm" + x, c, c + d), V(kn, kl, kl + d), u, A.is_le)
+            if m < 3:
+                ts(V("cm" + x, c + d + 32, c + 128), V(kn, kl + d + 32, kl + 128), u, A.is_lt)
+            ts(V("cm" + x, c + d, c + d + 32), V("kd" + x, d, d + 32), V("k4" + x, m, m + 1), A.is_lt)
+
+        def total():
+            for m in (1, 2, 0, 3):
+                scan(V("cs" + x, 128 * m, 128 * m + 128), V("ones", 0, 128), V("cm" + x, 128 * m, 128 * m + 128))
+        return [turn, second] + [lambda m=m: run(m) for m in (1, 2, 0, 3)] + [total]
+
+    def listed(t, cnt, val):
+        for m in range(4):
+            ts(V3("hb", 32 * m, 32 * m + 32), J3, cnt(m), A.is_equal, val(m), A.mult)
+        gap()
+        for j in (1, 0):
+            tr(H("ht", j, 0, 128), H("hb", j, 0, 128))
+        gap()
+        for j in (1, 0):
+            most(V("lbu", 2 * t + j, 2 * t + j + 1), H("ht", j, 0, 128))
+
+    def send(t):
+        d = T.cores[rank ^ [1, 2, 4, 1, 2][t]]
+        rid, pid = topo.addr(d, core)
+        es = topo.engines(core, d)[:8]
+        n = len(es) // 2
+        a = 128 + 32 * t if t < 4 else 128
+        waits("g", [("out%d" % t, 0, 32), ("ous%d" % t, 0, 128)], [])
+        to = [DstId(rid=rid, pnc=pid)]
+        g.remote_dma_fused([
+            RemoteDMATransfer(dst_ids=to, dma_engine_mask=sum(1 << e for e in es[:n]), remote_sem=T.sem["arr%d" % t],
+                              srcs=[T["out%d" % t][:, 0:32].bitcast(dt.uint8)], dsts=[T["win%d" % (t + 1)][:, a:a + 32].bitcast(dt.uint8)]),
+            RemoteDMATransfer(dst_ids=to, dma_engine_mask=sum(1 << e for e in es[n:]), remote_sem=T.sem["arr%d" % t],
+                              srcs=[T["ous%d" % t][:, 0:128]], dsts=[T["wis%d" % (t + 1)][:, a:a + 128]])],
+            local_sem=T.sem["snd%d" % t])
+        ends["snd%d" % t] = ends["arr%d" % t] = 2 * n
+        wr.setdefault("win%d" % (t + 1), []).append((a, a + 32, "x", "arr%d" % t, 2 * n))
+        wr.setdefault("wis%d" % (t + 1), []).append((a, a + 128, "x", "arr%d" % t, 2 * n))
+
+    def pick(t, off):
+        w = WW[t]
+        cp(C32(V("out%d" % t, 0, 32)), IX(C32(V("win%d" % t, 0, w)), off))
+        act(V("ous%d" % t, 0, 32), IX(V("wis%d" % t, 0, w), off), F.Copy)
+        send(t)
+
+    PA, PAC = V("pa", 0, 32), V("pac", 0, 32)
+
+    def AF(q, t):
+        i = 32 * (5 * t + q)
+        return V("af", i, i + 32)
+
+    def head(t):
+        b = mm("rq", "rs", 128 * t, "win%d" % t, "wis%d" % t, 32 * t)
+        square(AF(t, t - 1), b, 96, 128)
+
+    def floor(t):
+        ts(V("xa", 0, 32), AF(t, t - 1), TINY, A.max)
+
+    def turned():
+        tr(V("at", 0, 32), V("xa", 0, 32))
+        tt(V("xm", 32, 64), V("xa", 0, 32), V("fa", 0, 32), A.mult)
+
+    def stays(t, extra=()):
+        x = str(t % 2)
+        left = len(fillers)
+        act(PA, IX(V("qrow", 0, 128), LP(t - 1)), F.Copy)
+        gap(left - 1)
+        scatter(V("rv", 0, 128), LP(t - 1), V("zeros", 0, 32))
+        tr(PAC, PA)
+        gap()
+        for m in range(4):
+            act(V("gj", 32 * m, 32 * m + 32), IX(V("cm" + x, 128 * m, 128 * m + 128), LP(t - 1)), F.Copy, accum_out=V("lf", m, m + 1))
+        for e in extra:
+            later(*e)
+        tr(V("vc", 0, 128), V("rv", 0, 128))
+        ts(V("tf", 0, 128), V("qrow", 0, 128), V("pac", 0, 1), A.is_ge, PREV, A.max)
+        gap()
+        ts(V("fa", 0, 32), PA, V("pac", 0, 1), A.is_ge, PREV, A.max)
+        tt(V("tm", 0, 128), V("km" + x, 0, 128), V("tf", 0, 128), A.mult)
+        tt(V("cnt", 0, 4), V("cs" + x, 127, 512, 128), V("lf", 0, 4), A.subtract)
+        gap()
+        listed(t, lambda m: V("cnt", m, m + 1), lambda m: V("vc", 32 * m, 32 * m + 1))
+        gap()
+        if t > 1:
+            head(t)
+        act(V("pb", 0, 32), IX(V("qrow", 0, 128), LB(t)), F.Copy)
+        act(V("svb", 0, 32), IX(V("sv", 0, 128), LB(t)), F.Copy)
+        cp(V("xm", 0, 32), IX(V("tm", 0, 128), LB(t)))
+        if t > 1:
+            floor(t)
+        gap(9)
+        tr(V("tx", 0, 32), V("xm", 0, 32))
+        if t > 1:
+            turned()
+        tr(V("pbc", 0, 32), V("pb", 0, 32))
+        tr(V("svc", 0, 32), V("svb", 0, 32))
+
+    def YB(t, o):
+        return V("yy", 256 * t + 128 * o, 256 * t + 128 * o + 128)
+
+    def own():
+        for o in range(O):
+            b = mm("wq", "ws", 128 * o, "win0", "wis0", 0)
+            act(YB(1, o), PS(b, 0, 128), F.Copy)
+
+    def lay(t, o):
+        scatter(YB(t + 1, o), LP(t), V("zl", 128 * o + 32 * t, 128 * o + 32 * t + 32))
+        act(YB(t + 2, o), YB(t + 1, o), F.Copy)
+        if o == 1:
+            dma("s", "dy%d" % t, (T.y[:, 256 * t:256 * t + 256], T.yy[:, 256 * t + 256:256 * t + 512],
+                                  [("yy", 256 * t + 256, 256 * t + 512)], []))
+
+    def merge(t):
+        a = AF(t, t - 1)
+        if t == 1:
+            head(t)
+        more = [mm("rq", "rs", 128 * q, "win%d" % t, "wis%d" % t, 32 * t) for q in range(t + 1, 5)]
+        for q in range(t + 1, 5):
+            square(AF(q, t - 1), more[q - t - 1], 96, 128)
+        if t < 4:
+            dma("s", "dg%d" % (t + 1), *move(t, t + 1, 128, 128 + 32 * t))
+            act(V("rv", 0, 128), V("qrow", 0, 128), F.Copy)
+            later(tt, V("asum", 0, 32), a, AF(t + 1, t - 1), A.add)
+            later(scatter, KK(t + 1), LP(t - 1), V("asum", 0, 32))
+            fillers.extend(compare(t + 1, KK(t + 1)))
+        else:
+            for o in range(O):
+                b = mm("wq", "ws", 128 * o, "win4", "wis4", 128)
+                act(V("zl", 128 * o, 128 * o + 128), PS(b, 0, 128), F.Copy)
+            for u in range(4):
+                for o in range(O):
+                    for _ in range(1 if u + o else 2):
+                        later(lambda: None)
+                    later(lay, u, o)
+        if t == 1:
+            floor(t)
+        if t < 4:
+            scatter(V("sv", 0, 128), LP(t - 1), V("slr", 32 * (t - 1), 32 * t))
+        if t == 1:
+            turned()
+        tt(V("gm", 64, 96), V("xa", 0, 32), V("tx", 0, 32), A.is_le)
+        gap()
+        ts(V("gm", 0, 64), V("xm", 0, 64), V("at", 0, 1), A.is_lt)
+        gap()
+        scan(V("gs", 0, 96), V("rmc", 0, 96), V("gm", 0, 96))
+        gap()
+        s0, s1, col = V("gs", 95, 96), V("gs", 63, 64), 32 * (t - 1)
+        ts(V3("hc", 0, 32), JS, s0, A.is_equal, V("svc", 0, 1), A.mult)
+        ts(V3("hc", 32, 64), J3, s1, A.is_equal, V("pts", col, col + 1), A.mult)
+        ts(V3("hp", 0, 32), JS, s0, A.is_equal, V("pbc", 0, 1), A.mult)
+        ts(V3("hp", 32, 64), J3, s1, A.is_equal, V("pac", 0, 1), A.mult)
+        gap()
+        for j in range(2):
+            tr(H("hd", j, 0, 64), H("hc", j, 0, 64))
+        for j in range(2):
+            tr(H("hq", j, 0, 64), H("hp", j, 0, 64))
+        gap()
+        for j in range(2):
+            most(V("plu", 2 * t + j, 2 * t + j + 1), H("hd", j, 0, 64))
+        for j in range(2):
+            most(V("lpu", 2 * t + j, 2 * t + j + 1), H("hq", j, 0, 64))
+        gap()
+        pick(t, V("plu", 2 * t, 2 * t + 2))
+
+    for e in range(4):
+        rep(0, e, "v")
+    quant("win0", "wis0", 0, 128, V("cb", 0, 512))
+    quant("rq", "rs", 0, 128, RB(0, 1))
+    for e in range(4):
+        rep(1, e, "a")
+    b0 = mm("rq", "rs", 0, "win0", "wis0", 0)
+    square(V("sq", 0, 128), b0, 0, 128)
+    dma("s", "do", *[(T["ous%d" % t][:, 32:128], T.wis0[:, 32:128], [("wis0", 32, 128)], [("ous%d" % t, 32, 128)]) for t in range(5)])
+    for t in range(1, 6):
+        dma("s", "dn%d" % t, *move(0, t, 0, 128))
+    quant("rq", "rs", 128, 256, RB(1, 2))
+    b1 = mm("rq", "rs", 128, "win0", "wis0", 0)
+    square(V("sq", 128, 256), b1, 0, 128)
+    for t in range(2, 5):
+        for e in range(4):
+            rep(t, e, "a")
+    later(fill, V("rmc", 0, 1), 0.0)
+    later(tt, KK(1), SQ(0), SQ(1), A.add)
+    later(fill, V("rmc", 64, 65), 0.0)
+    fillers.extend(compare(1, KK(1)))
+    act(V("rv", 0, 128), V("qrow", 0, 128), F.Copy)
+    act(V("sv", 0, 128), V("qrow", 0, 128), F.Copy)
+    for step in compare(0, SQ(0)):
+        step()
+        gap()
+    listed(0, lambda m: V("cs0", 128 * m + 127, 128 * m + 128), lambda m: V("ptb", 32 * m, 32 * m + 1))
+    pick(0, LB(0))
+    quant("rq", "rs", 256, 640, RB(2, 5))
+    stays(1, [(ts, JS, J3, V("pt", 0, 1), A.subtract),
+              (ts, V("pts", 0, 128), V("pt", 0, 128), 128.0, A.add),
+              (ts, V("slr", 0, 128), V("qrow", 0, 128), 128.0, A.add)])
+    for t in range(2, 5):
+        b = mm("rq", "rs", 128 * t, "win0", "wis0", 0)
+        square(SQ(t), b, 0, 128)
+    tt(KK(2), KK(1), SQ(2), A.add)
+
+    for t in range(1, 4):
+        merge(t)
+        extra = []
+        if t < 3:
+            for q in range(t + 2, 5):
+                extra.append((scatter, SQ(q), LP(t - 1), AF(q, t - 1)))
+            extra.append((tt, KK(t + 2), KK(t + 1), SQ(t + 2), A.add))
+        if t == 2:
+            extra.append((quant, "wq", "ws", 0, 256, V("wb", 0, 1024)))
+        if t == 3:
+            extra.append((own,))
+        stays(t + 1, extra)
+    merge(4)
+
+    gap(99)
+    bs = [mm("wq", "ws", 128 * o, "win5", "wis5", 32) for o in range(O)]
+    act(V("zf", 0, 32), PS(bs[0], 96, 128), F.Copy)
+    cp(V("zf", 32, 64), PS(bs[1], 96, 128))
+    for o in range(O):
+        scatter(YB(5, o), LP(4), V("zf", 32 * o, 32 * o + 32))
+        dma("s" if o == 0 else "a", "dy%d" % (4 + o), (T.y[:, 1024 + 128 * o:1152 + 128 * o],
+            T.yy[:, 1280 + 128 * o:1408 + 128 * o], YB(5, o)[1], []))
+    for q in ("v", "a", "t", "g"):
+        wait("g", csem[q], count[q])
+    for s in sorted(ends):
+        wait("g", s, ends[s])

@@ -1,11 +1,11 @@
 from concourse.bass import DstId, RemoteDMATransfer
-from concourse.mybir import dt, AluOpType, AxisListType, ActivationFunctionType
+from concourse.mybir import dt, AluOpType, ActivationFunctionType
 
 P, K, R, O = 128, 32, 5, 2
 PREV = 1.0 - 2.0 ** -24
 TINY = 2.0 ** -121
 
-F4, BF, U16, CODE, PLANE = "float32", "bfloat16", "uint16", "float8_e4m3fn_x4", "uint8"
+F4, BF, U16, I32, CODE, PLANE = "float32", "bfloat16", "uint16", "int32", "float8_e4m3fn_x4", "uint8"
 WW = [128, 160, 192, 224, 256, 160]
 
 
@@ -14,15 +14,14 @@ def sb(kind, **widths):
 
 
 SCRATCH = {"ps": ("psum", [128, 4096], F4)}
-SCRATCH.update(sb(BF, cb=512, qb=20, wb=1024, rb=2560, ptb=128, ones=128, zeros=128, rmc=96, cnt=4,
-                  cm0=512, cm1=512, cs0=512, cs1=512, gj=128, rv=128, vc=128, hb=[2, 128], ht=[2, 128], gm=96,
-                  hc=[2, 64], hd=[2, 64], hp=[2, 64], hq=[2, 64]))
-SCRATCH.update(sb(F4, qrow=128, q32=128, pt=128, pts=128, slr=128, fd=128, j3=[2, 32], js=[2, 32],
-                  sq=640, kk=640, sv=128, km0=128, kt0=128, kd0=128, k40=4, km1=128, kt1=128, kd1=128, k41=4,
-                  lf=4, tf=128, tm=128, tx=32, pb=32, pbc=32, pa=32, pac=32, fa=32, xm=64, svb=32, svc=32,
-                  af=800, asum=32, xa=32, at=32, gs=96, zl=256, zf=64, yy=1536))
-SCRATCH.update(sb(U16, lbu=10, plu=10, lpu=10))
-SCRATCH.update(sb(CODE, rq=640, wq=256))
+SCRATCH.update(sb(BF, cb=512, qb=20, wb=1024, rb=2560, ones=160, zeros=512, cm=160, cs=160, j3=[2, 32], pay=5, nz=2,
+                  oh0=[2, 64], oh1=[2, 64], ht0=[2, 128], ht1=[2, 128]))
+SCRATCH.update(sb(F4, onef=128, zerof=32, fd=128, fn=128, s0=256, f0=256, j33=33, ab=33, sg=33, col=4,
+                  sq=640, kk=640, km=640, xa=320, uc=33, fa=64, dg=32, dc=32, ua=[4, 258], sn=96, uf=96,
+                  zl=256, zf=64, yy=1280))
+SCRATCH.update(sb(I32, pi=1, pj=1))
+SCRATCH.update(sb(U16, dl=2, ls=2560))
+SCRATCH.update(sb(CODE, rq=640, wq=256, zq=128))
 SCRATCH.update(sb(PLANE, rs=640, ws=256))
 for _t in range(6):
     _w = WW[_t] + (96 if _t else 0)
@@ -57,29 +56,32 @@ def rank_program(g, core, T, topo):
             if known[q].get(s, 0) < v:
                 known[q][s] = v
 
+    def meet(x, y):
+        return x[1] < y[2] and y[1] < x[2] and x[3] < y[4] and y[3] < x[4] and (x[5] == y[5] or None in (x[5], y[5]))
+
+    def inside(x, y):
+        return y[1] <= x[1] and x[2] <= y[2] and y[3] <= x[3] and x[4] <= y[4] and y[5] in (None, x[5])
+
     def waits(q, reads, writes):
         need = {}
-        for (n, lo, hi) in reads:
-            for (l, h, q2, s, v) in wr.get(n, ()):
-                if l < hi and lo < h:
+        for x in reads + writes:
+            for (y, q2, s, v) in wr.get(x[0], ()):
+                if meet(x, y):
                     need[s] = max(need.get(s, 0), v)
-        for (n, lo, hi) in writes:
-            for (l, h, q2, s, v) in wr.get(n, ()):
-                if l < hi and lo < h:
-                    need[s] = max(need.get(s, 0), v)
-            for (l, h, q2, s, v) in rd.get(n, ()):
-                if l < hi and lo < h and (q2 != q or s[0] == "d"):
+        for x in writes:
+            for (y, q2, s, v) in rd.get(x[0], ()):
+                if meet(x, y) and (q2 != q or s[0] == "d"):
                     need[s] = max(need.get(s, 0), v)
         for s in sorted(need):
             wait(q, s, need[s])
 
     def note(q, reads, writes, sem, val):
         snap[(sem, val)] = dict(known[q])
-        for (n, lo, hi) in writes:
-            wr[n] = [e for e in wr.get(n, ()) if not (lo <= e[0] and e[1] <= hi)] + [(lo, hi, q, sem, val)]
-            rd[n] = [e for e in rd.get(n, ()) if not (lo <= e[0] and e[1] <= hi)]
-        for (n, lo, hi) in reads:
-            rd.setdefault(n, []).append((lo, hi, q, sem, val))
+        for x in writes:
+            wr[x[0]] = [e for e in wr.get(x[0], ()) if not inside(e[0], x)] + [(x, q, sem, val)]
+            rd[x[0]] = [e for e in rd.get(x[0], ()) if not inside(e[0], x)]
+        for x in reads:
+            rd.setdefault(x[0], []).append((x, q, sem, val))
 
     def op(q, fn, reads, writes):
         waits(q, reads, writes)
@@ -89,27 +91,30 @@ def rank_program(g, core, T, topo):
         note(q, reads, writes, csem[q], count[q])
 
     def dma(q, sem, *moves):
-        for (out, in_, reads, writes) in moves:
-            waits(q, reads, writes)
-            eng[q].dma_start(out, in_).then_inc(T.sem[sem], 16)
+        for (out, in_) in moves:
+            waits(q, rg(in_), rg(out))
+            eng[q].dma_start(ap(out), ap(in_)).then_inc(T.sem[sem], 16)
         ends[sem] = 16 * len(moves)
-        for (out, in_, reads, writes) in moves:
-            note(q, reads, writes, sem, ends[sem])
+        for (out, in_) in moves:
+            note(q, rg(in_), rg(out), sem, ends[sem])
 
-    def V(n, a, b, step=1):
-        return (T[n][:, a:b] if step == 1 else T[n][:, a:b:step], [(n, a, b)])
+    ALL, LO, HI, B0, B1 = (0, 128), (0, 64), (64, 128), (0, 32), (32, 64)
 
-    def V3(n, a, b):
-        return (T[n][:, :, a:b], [(n + "0", a, b), (n + "1", a, b)])
-
-    def H(n, j, a, b):
-        return (T[n][:, j, a:b], [(n + str(j), a, b)])
+    def V(n, a, b, step=1, part=ALL, half=None):
+        cols = slice(a, b) if step == 1 else slice(a, b, step)
+        rows = slice(None) if part == ALL else slice(part[0], part[1])
+        odd = a % 2 if step == 2 else None
+        if half is None:
+            return (T[n][rows, cols], [(n, a, b, part[0], part[1], odd)])
+        if half == "all":
+            return (T[n][rows, :, cols], [(n + "/%d" % j, a, b, part[0], part[1], odd) for j in range(T[n].shape[1])])
+        return (T[n][rows, half, cols], [(n + "/%d" % half, a, b, part[0], part[1], odd)])
 
     def IX(v, off):
         return (v[0].indirect(off[0]), v[1] + off[1])
 
-    def C32(v):
-        return (v[0].bitcast(dt.uint32), v[1])
+    def AS(v, d):
+        return (v[0].bitcast(d), v[1])
 
     def ap(x):
         return x[0] if isinstance(x, tuple) else x
@@ -139,10 +144,7 @@ def rank_program(g, core, T, topo):
     def tr(out, in_):
         op("v", lambda: g.vector.transpose(ap(out), ap(in_)), rg(in_), rg(out))
 
-    def most(out, in_):
-        op("v", lambda: g.vector.tensor_reduce(ap(out), ap(in_), AxisListType.X, A.max), rg(in_), rg(out))
-
-    def scan(out, d0, d1, start=0.0, o=A.add):
+    def scan(out, d0, d1, start, o):
         op("v", lambda: g.vector.tensor_tensor_scan(ap(out), ap(d0), ap(d1), ap(start), A.mult, o), rg(d0, d1, start), rg(out))
 
     def fill(v, c):
@@ -153,9 +155,7 @@ def rank_program(g, core, T, topo):
         op("v", lambda: g.vector.quantize_mx(x[0], y[0], ap(in_)), rg(in_), rg(x, y))
 
     def act(out, in_, f, **kw):
-        more = [kw["accum_out"]] if "accum_out" in kw else []
-        op("a", lambda: g.scalar.activation(ap(out), ap(in_), f, **{k: ap(kw[k]) for k in kw}),
-           rg(in_, *[kw[k] for k in kw if k != "accum_out"]), rg(out, *more))
+        op("a", lambda: g.scalar.activation(ap(out), ap(in_), f, **{k: ap(kw[k]) for k in kw}), rg(in_, *kw.values()), rg(out))
 
     bank = [0]
 
@@ -163,102 +163,78 @@ def rank_program(g, core, T, topo):
         b = 512 * (bank[0] % 8)
         bank[0] += 1
         l, m, r, s = V(lq, la, la + 128), V(ls, la, la + 128), V(rq, ra, ra + 128), V(rs, ra, ra + 128)
-        op("t", lambda: g.tensor.matmul_mx(T.ps[:, b:b + 128], l[0], m[0], r[0], s[0], True, True), rg(l, m, r, s), [("ps", b, b + 512)])
+        op("t", lambda: g.tensor.matmul_mx(T.ps[:, b:b + 128], l[0], m[0], r[0], s[0], True, True), rg(l, m, r, s), rg(V("ps", b, b + 512)))
         return b
 
     def PS(b, lo, hi):
-        return (T.ps[:, b + lo:b + hi], [("ps", b, b + 512)])
+        return (T.ps[:, b + lo:b + hi], rg(V("ps", b, b + 512)))
 
-    def iota(v, pattern):
-        op("g", lambda: g.iota(v[0], pattern, 0, 0, allow_small_or_imprecise_dtypes=True), [], v[1])
+    def iota(v, pattern, cm=0):
+        if v[1][0][0] == "pi":
+            op("g", lambda: g.iota(v[0], pattern, 0, cm), [], v[1])
+        else:
+            op("g", lambda: g.iota(v[0], pattern, 0, cm, allow_small_or_imprecise_dtypes=True), [], v[1])
 
     fillers = []
 
-    def later(f, *args):
-        fillers.append(lambda: f(*args))
+    def later(*calls):
+        fillers.append(calls)
 
     def gap(k=1):
         for _ in range(k):
-            if fillers:
-                fillers.pop(0)()
+            for c in (fillers.pop(0) if fillers else ()):
+                c[0](*c[1:])
 
-    dma("a", "dq", (T.qb[:, 0:20], T.qt[:, 0:20], [], [("qb", 0, 20)]))
-    dma("s", "dc", (T.cb[:, 0:512], T.c[:, 0:512], [], [("cb", 0, 512)]))
-    dma("s", "dw", (T.wb[:, 0:1024], T.w[:, 0:1024], [], [("wb", 0, 1024)]))
-    iota(V("qrow", 0, 128), [[1, 128]])
-    iota(V("q32", 0, 128), [[0, 4], [1, 32]])
-    J3, JS = (T.j3[:, :, :], [("j3", 0, 32)]), (T.js[:, :, :], [("js", 0, 32)])
-    iota(J3, [[16, 2], [0, 2], [1, 16]])
-    fill(V("zeros", 0, 128), 0.0)
-    fill(V("ones", 0, 128), 1.0)
-    fill(V("rmc", 0, 96), 1.0)
-    tr(V("pt", 0, 128), V("qrow", 0, 128))
-    ts(V("fd", 0, 128), V("q32", 0, 128), V("pt", 0, 1), A.is_ge, PREV, A.max)
-    cp(V("ptb", 0, 128), V("pt", 0, 128))
+    dma("a", "dq", (V("qb", 0, 20), T.qt[:, 0:20]))
+    dma("s", "dc", (V("cb", 0, 512), T.c[:, 0:512]))
+    ONE = V("onef", 0, 128)
+    fill(ONE, 1.0)
+    iota(V("pi", 0, 1), [[0, 1]], 1)
+    op("g", lambda: g.affine_select(T.fd[:, 0:128], ONE[0], [[1, 128]], A.is_ge, PREV, 0, -1), ONE[1], rg(V("fd", 0, 128)))
+    iota(V("j3", 0, 32, half="all"), [[16, 2], [0, 2], [1, 16]])
+    iota(V("pay", 0, 1), [[0, 1]], 1)
+    iota(V("j33", 0, 33), [[1, 33]])
+    fill(V("zeros", 0, 512), 0.0)
+    fill(V("ones", 0, 160), 1.0)
+    fill(V("s0", 0, 256, 2), 0.0)
+    quant("zq", "ous0", 0, 128, V("zeros", 0, 512))
+    fill(V("zerof", 0, 32), 0.0)
+    fill(V("ua", 192, 256, 2, half="all"), 0.0)
+    fill(V("ua", 257, 258, half="all"), -TINY)
+    ts(V("pj", 0, 1), V("pi", 0, 1), 128 - 1 - 16, A.bitwise_and)
+    cp(V("f0", 0, 256, 2), V("fd", 0, 128))
+    ts(V("f0", 1, 256, 2), V("fd", 0, 128), TINY, A.mult)
+    for c in range(2):
+        ts(V("dl", c, c + 1), V("pj", 0, 1), 16.0 * c, A.add)
+    act(V("fn", 0, 128), V("fd", 0, 128), F.Copy, scale=-1.0)
+    fill(V("j33", 32, 33), 31.5)
 
-    def rep(t, e, on):
-        o, q = (T.rb[:, 512 * t + e:512 * t + 512:4], [("rb%d" % e, t, t + 1)]), V("qb", 4 * t + e, 4 * t + e + 1)
-        if on == "v":
-            ts(o, V("ones", 0, 128), q, A.mult)
-        else:
-            act(o, V("zeros", 0, 128), F.Identity, bias=q)
+    def rep(t, on):
+        for e in range(4):
+            o, q = (T.rb[:, 512 * t + e:512 * t + 512:4], [("rb%d" % e, t, t + 1, 0, 128, None)]), V("qb", 4 * t + e, 4 * t + e + 1)
+            if on == "v":
+                ts(o, V("ones", 0, 128), q, A.mult)
+            else:
+                act(o, V("zeros", 0, 128), F.Identity, bias=q)
 
-    def RB(t, u):
-        return (T.rb[:, 512 * t:512 * u], [("rb%d" % e, t, u) for e in range(4)])
+    def quantq(t):
+        quant("rq", "rs", 128 * t, 128 * t + 128, (T.rb[:, 512 * t:512 * t + 512], [("rb%d" % e, t, t + 1, 0, 128, None) for e in range(4)]))
 
     def square(dst, b, lo, hi):
         act(dst, PS(b, lo, hi), F.Square)
 
     def move(m, n, a, b):
-        x, y, s, r = V("win%d" % n, a, b), V("win%d" % m, a, b), V("wis%d" % n, a, b), V("wis%d" % m, a, b)
-        return ((x[0].bitcast(dt.uint8), y[0].bitcast(dt.uint8), y[1], x[1]), (s[0], r[0], r[1], s[1]))
+        return ((AS(V("win%d" % n, a, b), dt.uint8), AS(V("win%d" % m, a, b), dt.uint8)), (V("wis%d" % n, a, b), V("wis%d" % m, a, b)))
 
-    def SQ(t):
-        return V("sq", 128 * t, 128 * t + 128)
+    def row(n, t):
+        return V(n, 128 * t, 128 * t + 128)
 
-    def KK(t):
-        return V("kk", 128 * t, 128 * t + 128)
+    def LIST(t, i):
+        a = 512 * t + 256 * (i if t else 0) + 254
+        return V("ls", a, a + 2)
 
-    def LB(t):
-        return V("lbu", 2 * t, 2 * t + 2)
-
-    def LP(t):
-        return V("lpu" if t else "lbu", 2 * t, 2 * t + 2)
-
-    def compare(t, k):
-        x = str(t % 2)
-        kn, kl = k[1][0][0], k[1][0][1]
-
-        def turn():
-            tr(V("kt" + x, 0, 128), k)
-            ts(V("km" + x, 0, 128), k, TINY, A.max)
-
-        def second():
-            tt(V("kd" + x, 0, 128), V("km" + x, 0, 128), V("fd", 0, 128), A.mult)
-            ts(V("k4" + x, 0, 4), V("kt" + x, 0, 128, 32), TINY, A.max)
-
-        def run(m):
-            u, c, d = V("kt" + x, 32 * m, 32 * m + 1), 128 * m, 32 * m
-            if m > 0:
-                ts(V("cm" + x, c, c + d), V(kn, kl, kl + d), u, A.is_le)
-            if m < 3:
-                ts(V("cm" + x, c + d + 32, c + 128), V(kn, kl + d + 32, kl + 128), u, A.is_lt)
-            ts(V("cm" + x, c + d, c + d + 32), V("kd" + x, d, d + 32), V("k4" + x, m, m + 1), A.is_lt)
-
-        def total():
-            for m in (1, 2, 0, 3):
-                scan(V("cs" + x, 128 * m, 128 * m + 128), V("ones", 0, 128), V("cm" + x, 128 * m, 128 * m + 128))
-        return [turn, second] + [lambda m=m: run(m) for m in (1, 2, 0, 3)] + [total]
-
-    def listed(t, cnt, val):
-        for m in range(4):
-            ts(V3("hb", 32 * m, 32 * m + 32), J3, cnt(m), A.is_equal, val(m), A.mult)
-        gap()
-        for j in (1, 0):
-            tr(H("ht", j, 0, 128), H("hb", j, 0, 128))
-        gap()
-        for j in (1, 0):
-            most(V("lbu", 2 * t + j, 2 * t + j + 1), H("ht", j, 0, 128))
+    def RANK(t):
+        return V("cs", 159, 160) if t else V("cs", 127, 128)
 
     def send(t):
         d = T.cores[rank ^ [1, 2, 4, 1, 2][t]]
@@ -266,7 +242,7 @@ def rank_program(g, core, T, topo):
         es = topo.engines(core, d)[:8]
         n = len(es) // 2
         a = 128 + 32 * t if t < 4 else 128
-        waits("g", [("out%d" % t, 0, 32), ("ous%d" % t, 0, 128)], [])
+        waits("g", rg(V("out%d" % t, 0, 32), V("ous%d" % t, 0, 128)), [])
         to = [DstId(rid=rid, pnc=pid)]
         g.remote_dma_fused([
             RemoteDMATransfer(dst_ids=to, dma_engine_mask=sum(1 << e for e in es[:n]), remote_sem=T.sem["arr%d" % t],
@@ -275,193 +251,179 @@ def rank_program(g, core, T, topo):
                               srcs=[T["ous%d" % t][:, 0:128]], dsts=[T["wis%d" % (t + 1)][:, a:a + 128]])],
             local_sem=T.sem["snd%d" % t])
         ends["snd%d" % t] = ends["arr%d" % t] = 2 * n
-        wr.setdefault("win%d" % (t + 1), []).append((a, a + 32, "x", "arr%d" % t, 2 * n))
-        wr.setdefault("wis%d" % (t + 1), []).append((a, a + 128, "x", "arr%d" % t, 2 * n))
+        wr.setdefault("win%d" % (t + 1), []).append((rg(V("win%d" % (t + 1), a, a + 32))[0], "x", "arr%d" % t, 2 * n))
+        wr.setdefault("wis%d" % (t + 1), []).append((rg(V("wis%d" % (t + 1), a, a + 128))[0], "x", "arr%d" % t, 2 * n))
 
-    def pick(t, off):
+    def mark(t, i):
+        for c, h in ((0, LO), (32, HI)):
+            ts(V("oh%d" % i, c, c + 32, part=LO, half="all"), V("j3", 0, 32, part=h, half="all"), V("cs", RANK(t)[1][0][1], RANK(t)[1][0][2], part=h),
+               A.is_equal, V("pay", 0 if i else t, 1 if i else t + 1, part=h), A.mult)
+
+    def turn(i):
+        for c, to, h in ((0, LO, LO), (64, B1, B0), (64, B0, B1)):
+            tr(V("ht%d" % i, c, c + 64, part=to, half="all"), V("oh%d" % i, 0, 64, part=h, half="all"))
+
+    def gather(t, i, h):
+        a = 512 * t + 256 * i
+        for j in range(2):
+            scan(V("ls", a + j, a + 256, 2, part=h), V("ones", 0, 128, part=LO), V("ht%d" % i, 0, 128, part=LO, half=j), 0.0, A.max)
+
+    def leave(t):
+        n = 160 if t else 128
+        ts(V("cm", 0, n), V("xa", 1, 2 * n, 2), V("uc", 32, 33), A.is_gt if t else A.is_lt)
+        gap()
+        scan(V("cs", 0, n), V("ones", 0, n), V("cm", 0, n), -32.0 if t else 0.0, A.add)
+        gap()
+        mark(t, 0)
+        if t < 4:
+            signs(t)
+        mark(t, 1) if t else gap()
+        turn(0)
+        turn(1) if t else gap()
+        gather(t, 0, LO)
+        gather(t, 0, HI)
+        gather(t, 1, LO) if t else gap()
         w = WW[t]
-        cp(C32(V("out%d" % t, 0, 32)), IX(C32(V("win%d" % t, 0, w)), off))
-        act(V("ous%d" % t, 0, 32), IX(V("wis%d" % t, 0, w), off), F.Copy)
+        act(V("ous%d" % t, 0, 32), IX(V("wis%d" % t, 0, w), LIST(t, 0)), F.Copy)
+        cp(AS(V("out%d" % t, 0, 32), dt.uint32), IX(AS(V("win%d" % t, 0, w), dt.uint32), LIST(t, 0)))
         send(t)
+        if t:
+            gather(t, 1, HI)
+        gap(99)
 
-    PA, PAC = V("pa", 0, 32), V("pac", 0, 32)
+    def signs(t):
+        r = RANK(t)
+        act(V("col", 0, 1), r, F.Identity, scale=-1.0, bias=-0.5)
+        act(V("nz", 0, 1), r, F.Identity, bias=128.0 + 32 * t)
+        act(V("ab", 0, 33), V("j33", 0, 33), F.Abs, bias=V("col", 0, 1))
+        act(V("nz", 1, 2), r, F.Identity, scale=-1000.0, bias=32000.0)
+        act(V("sg", 0, 33), V("ab", 0, 33), F.Sign, bias=-0.75)
+        act(V("col", 1, 2), r, F.Relu, scale=-1e18, bias=31.5e18)
 
-    def AF(q, t):
-        i = 32 * (5 * t + q)
-        return V("af", i, i + 32)
+    def ready(t):
+        lp = LIST(t - 1, 1)
+        act(V("fa", 0, 64, 2), IX(V("fn", 0, 128), lp), F.Copy)
+        act(V("fa", 1, 64, 2), IX(V("fn", 0, 128), lp), F.Copy, scale=TINY)
+        ts(V("pay", t, t + 1), V("nz", 0, 1), V("nz", 1, 2), A.min, V("pay", t - 1, t), A.max)
+        for s in range(1, t - 1):
+            older(t, s)
+            gap()
+        scatter(row("km", t), lp, V("zerof", 0, 32))
+        act(V("dg", 0, 32), IX(row("km", t), V("dl", 0, 2)), F.Copy)
+        gap()
+        tt(V("xa", 1, 256, 2), row("km", t), V("fn", 0, 128), A.mult)
+        tr(V("dc", 0, 32), V("dg", 0, 32))
+        gap()
+        ts(V("col", 2, 3), V("col", 1, 2), -5e18, A.mult, V("dc", 0, 1), A.subtract)
+        gap(99)
 
-    def head(t):
-        b = mm("rq", "rs", 128 * t, "win%d" % t, "wis%d" % t, 32 * t)
-        square(AF(t, t - 1), b, 96, 128)
+    def own(t):
+        square(row("sq", t), mm("rq", "rs", 128 * t, "win0", "wis0", 0), 0, 128)
+
+    def uses(t):
+        tt(row("kk", t), row("kk", t - 1) if t > 1 else V("s0", 1, 256, 2), row("sq", t), A.add)
 
     def floor(t):
-        ts(V("xa", 0, 32), AF(t, t - 1), TINY, A.max)
+        ts(row("km", t), row("kk", t), TINY, A.max)
 
-    def turned():
-        tr(V("at", 0, 32), V("xa", 0, 32))
-        tt(V("xm", 32, 64), V("xa", 0, 32), V("fa", 0, 32), A.mult)
-
-    def stays(t, extra=()):
-        x = str(t % 2)
-        left = len(fillers)
-        act(PA, IX(V("qrow", 0, 128), LP(t - 1)), F.Copy)
-        gap(left - 1)
-        scatter(V("rv", 0, 128), LP(t - 1), V("zeros", 0, 32))
-        tr(PAC, PA)
-        gap()
-        for m in range(4):
-            act(V("gj", 32 * m, 32 * m + 32), IX(V("cm" + x, 128 * m, 128 * m + 128), LP(t - 1)), F.Copy, accum_out=V("lf", m, m + 1))
-        for e in extra:
-            later(*e)
-        tr(V("vc", 0, 128), V("rv", 0, 128))
-        ts(V("tf", 0, 128), V("qrow", 0, 128), V("pac", 0, 1), A.is_ge, PREV, A.max)
-        gap()
-        ts(V("fa", 0, 32), PA, V("pac", 0, 1), A.is_ge, PREV, A.max)
-        tt(V("tm", 0, 128), V("km" + x, 0, 128), V("tf", 0, 128), A.mult)
-        tt(V("cnt", 0, 4), V("cs" + x, 127, 512, 128), V("lf", 0, 4), A.subtract)
-        gap()
-        listed(t, lambda m: V("cnt", m, m + 1), lambda m: V("vc", 32 * m, 32 * m + 1))
-        gap()
-        if t > 1:
-            head(t)
-        act(V("pb", 0, 32), IX(V("qrow", 0, 128), LB(t)), F.Copy)
-        act(V("svb", 0, 32), IX(V("sv", 0, 128), LB(t)), F.Copy)
-        cp(V("xm", 0, 32), IX(V("tm", 0, 128), LB(t)))
-        if t > 1:
-            floor(t)
-        gap(9)
-        tr(V("tx", 0, 32), V("xm", 0, 32))
-        if t > 1:
-            turned()
-        tr(V("pbc", 0, 32), V("pb", 0, 32))
-        tr(V("svc", 0, 32), V("svb", 0, 32))
+    def UA(t, a, b):
+        o = 128 - 32 * t
+        return V("ua", 2 * (o + a) + 1, 2 * (o + b), 2, half=t - 1)
 
     def YB(t, o):
         return V("yy", 256 * t + 128 * o, 256 * t + 128 * o + 128)
 
-    def own():
+    def under_w(win, a, lo, hi, dst):
         for o in range(O):
-            b = mm("wq", "ws", 128 * o, "win0", "wis0", 0)
-            act(YB(1, o), PS(b, 0, 128), F.Copy)
+            b = mm("wq", "ws", 128 * o, "win%d" % win, "wis%d" % win, a)
+            act(dst(o), PS(b, lo, hi), F.Copy)
 
     def lay(t, o):
-        scatter(YB(t + 1, o), LP(t), V("zl", 128 * o + 32 * t, 128 * o + 32 * t + 32))
-        act(YB(t + 2, o), YB(t + 1, o), F.Copy)
-        if o == 1:
-            dma("s", "dy%d" % t, (T.y[:, 256 * t:256 * t + 256], T.yy[:, 256 * t + 256:256 * t + 512],
-                                  [("yy", 256 * t + 256, 256 * t + 512)], []))
+        scatter(YB(t, o), LIST(t, 1), V("zl", 128 * o + 32 * t, 128 * o + 32 * t + 32))
 
-    def merge(t):
-        a = AF(t, t - 1)
-        if t == 1:
-            head(t)
-        more = [mm("rq", "rs", 128 * q, "win%d" % t, "wis%d" % t, 32 * t) for q in range(t + 1, 5)]
-        for q in range(t + 1, 5):
-            square(AF(q, t - 1), more[q - t - 1], 96, 128)
+    def keep(t):
+        for o in range(O):
+            act(YB(t + 1, o), YB(t, o), F.Copy)
+        dma("s", "dy%d" % t, (T.y[:, 256 * t:256 * t + 256], V("yy", 256 * t, 256 * t + 256)))
+
+    def older(t, s):
+        scatter(row("km", t), LIST(s, 1), V("uf", 32 * s, 32 * s + 32))
+
+    def landed(t):
+        w = ("win%d" % t, "wis%d" % t, 32 * t)
+        square(UA(t, 32 * t - 32, 32 * t), mm("rq", "rs", 128 * t, *w), 96, 128)
         if t < 4:
+            square(V("sn", 0, 32 * t), mm("rq", "rs", 128 * t + 128, *w), 128 - 32 * t, 128)
             dma("s", "dg%d" % (t + 1), *move(t, t + 1, 128, 128 + 32 * t))
-            act(V("rv", 0, 128), V("qrow", 0, 128), F.Copy)
-            later(tt, V("asum", 0, 32), a, AF(t + 1, t - 1), A.add)
-            later(scatter, KK(t + 1), LP(t - 1), V("asum", 0, 32))
-            fillers.extend(compare(t + 1, KK(t + 1)))
-        else:
-            for o in range(O):
-                b = mm("wq", "ws", 128 * o, "win4", "wis4", 128)
-                act(V("zl", 128 * o, 128 * o + 128), PS(b, 0, 128), F.Copy)
-            for u in range(4):
-                for o in range(O):
-                    for _ in range(1 if u + o else 2):
-                        later(lambda: None)
-                    later(lay, u, o)
-        if t == 1:
-            floor(t)
+        if t in (2, 4):
+            under_w(t, 32 * t, 64, 128, lambda o: V("zl", 128 * o + 32 * t - 64, 128 * o + 32 * t))
+        scan(V("uc", 0, 33), V("sg", 0, 33), V("ua", 193, 258, 2, half=t - 1), V("col", 2, 3), A.min)
+        scan(V("xa", 256, 320), V("ua", 192, 256, half=t - 1), V("fa", 0, 64), 0.0, A.min)
         if t < 4:
-            scatter(V("sv", 0, 128), LP(t - 1), V("slr", 32 * (t - 1), 32 * t))
-        if t == 1:
-            turned()
-        tt(V("gm", 64, 96), V("xa", 0, 32), V("tx", 0, 32), A.is_le)
-        gap()
-        ts(V("gm", 0, 64), V("xm", 0, 64), V("at", 0, 1), A.is_lt)
-        gap()
-        scan(V("gs", 0, 96), V("rmc", 0, 96), V("gm", 0, 96))
-        gap()
-        s0, s1, col = V("gs", 95, 96), V("gs", 63, 64), 32 * (t - 1)
-        ts(V3("hc", 0, 32), JS, s0, A.is_equal, V("svc", 0, 1), A.mult)
-        ts(V3("hc", 32, 64), J3, s1, A.is_equal, V("pts", col, col + 1), A.mult)
-        ts(V3("hp", 0, 32), JS, s0, A.is_equal, V("pbc", 0, 1), A.mult)
-        ts(V3("hp", 32, 64), J3, s1, A.is_equal, V("pac", 0, 1), A.mult)
-        gap()
-        for j in range(2):
-            tr(H("hd", j, 0, 64), H("hc", j, 0, 64))
-        for j in range(2):
-            tr(H("hq", j, 0, 64), H("hp", j, 0, 64))
-        gap()
-        for j in range(2):
-            most(V("plu", 2 * t + j, 2 * t + j + 1), H("hd", j, 0, 64))
-        for j in range(2):
-            most(V("lpu", 2 * t + j, 2 * t + j + 1), H("hq", j, 0, 64))
-        gap()
-        pick(t, V("plu", 2 * t, 2 * t + 2))
+            tt(UA(t + 1, 0, 32 * t), UA(t, 0, 32 * t), V("sn", 0, 32 * t), A.add)
+            later((ts, V("uf", 0, 32 * t), UA(t + 1, 0, 32 * t), TINY, A.max))
+            later((older, t + 1, 0))
 
-    for e in range(4):
-        rep(0, e, "v")
+    rep(0, "v")
     quant("win0", "wis0", 0, 128, V("cb", 0, 512))
-    quant("rq", "rs", 0, 128, RB(0, 1))
-    for e in range(4):
-        rep(1, e, "a")
-    b0 = mm("rq", "rs", 0, "win0", "wis0", 0)
-    square(V("sq", 0, 128), b0, 0, 128)
-    dma("s", "do", *[(T["ous%d" % t][:, 32:128], T.wis0[:, 32:128], [("wis0", 32, 128)], [("ous%d" % t, 32, 128)]) for t in range(5)])
+    quantq(0)
+    rep(1, "a")
+    square(V("s0", 1, 256, 2), mm("rq", "rs", 0, "win0", "wis0", 0), 0, 128)
+    b = mm("win0", "wis0", 0, "rq", "rs", 0)
     for t in range(1, 6):
         dma("s", "dn%d" % t, *move(0, t, 0, 128))
-    quant("rq", "rs", 128, 256, RB(1, 2))
-    b1 = mm("rq", "rs", 128, "win0", "wis0", 0)
-    square(V("sq", 128, 256), b1, 0, 128)
-    for t in range(2, 5):
-        for e in range(4):
-            rep(t, e, "a")
-    later(fill, V("rmc", 0, 1), 0.0)
-    later(tt, KK(1), SQ(0), SQ(1), A.add)
-    later(fill, V("rmc", 64, 65), 0.0)
-    fillers.extend(compare(1, KK(1)))
-    act(V("rv", 0, 128), V("qrow", 0, 128), F.Copy)
-    act(V("sv", 0, 128), V("qrow", 0, 128), F.Copy)
-    for step in compare(0, SQ(0)):
-        step()
-        gap()
-    listed(0, lambda m: V("cs0", 128 * m + 127, 128 * m + 128), lambda m: V("ptb", 32 * m, 32 * m + 1))
-    pick(0, LB(0))
-    quant("rq", "rs", 256, 640, RB(2, 5))
-    stays(1, [(ts, JS, J3, V("pt", 0, 1), A.subtract),
-              (ts, V("pts", 0, 128), V("pt", 0, 128), 128.0, A.add),
-              (ts, V("slr", 0, 128), V("qrow", 0, 128), 128.0, A.add)])
-    for t in range(2, 5):
-        b = mm("rq", "rs", 128 * t, "win0", "wis0", 0)
-        square(SQ(t), b, 0, 128)
-    tt(KK(2), KK(1), SQ(2), A.add)
-
-    for t in range(1, 4):
-        merge(t)
-        extra = []
-        if t < 3:
-            for q in range(t + 2, 5):
-                extra.append((scatter, SQ(q), LP(t - 1), AF(q, t - 1)))
-            extra.append((tt, KK(t + 2), KK(t + 1), SQ(t + 2), A.add))
-        if t == 2:
-            extra.append((quant, "wq", "ws", 0, 256, V("wb", 0, 1024)))
+    dma("s", "dw", (V("wb", 0, 1024), T.w[:, 0:1024]))
+    dma("s", "do", *[(V("ous%d" % t, 32, 128), V("wis0", 32, 128)) for t in range(1, 5)])
+    quantq(1)
+    own(1)
+    rep(2, "a")
+    ts(V("uc", 32, 33), PS(b, 0, 1), PS(b, 0, 1), A.mult, TINY, A.max)
+    scan(V("xa", 0, 256), V("s0", 0, 256), V("f0", 0, 256), 0.0, A.max)
+    later()
+    later()
+    later((uses, 1))
+    later((floor, 1))
+    later((quantq, 2))
+    leave(0)
+    later()
+    later((own, 2), (rep, 3, "a"), (quant, "wq", "ws", 0, 256, V("wb", 0, 1024)))
+    ready(1)
+    uses(2)
+    quantq(3)
+    own(3)
+    under_w(0, 0, 0, 128, lambda o: YB(0, o))
+    floor(2)
+    for t in range(1, 5):
+        landed(t)
+        if t == 1:
+            rep(4, "a")
         if t == 3:
-            extra.append((own,))
-        stays(t + 1, extra)
-    merge(4)
+            keep(0)
+        if t == 4:
+            later((lay, 1, 0))
+            later((lay, 1, 1), (keep, 1))
+        leave(t)
+        if t < 4:
+            if t == 1:
+                quantq(4)
+            if t < 3:
+                later((uses, t + 2))
+                later((floor, t + 2), *([(own, 4)] if t == 1 else []))
+            if t == 2:
+                later((lay, 0, 0))
+                later((lay, 0, 1))
+            ready(t + 1)
+    for t in (2, 3):
+        lay(t, 0)
+        lay(t, 1)
+        keep(t)
 
-    gap(99)
     bs = [mm("wq", "ws", 128 * o, "win5", "wis5", 32) for o in range(O)]
-    act(V("zf", 0, 32), PS(bs[0], 96, 128), F.Copy)
-    cp(V("zf", 32, 64), PS(bs[1], 96, 128))
+    cp(V("zf", 0, 32), PS(bs[0], 96, 128))
+    act(V("zf", 32, 64), PS(bs[1], 96, 128), F.Copy)
     for o in range(O):
-        scatter(YB(5, o), LP(4), V("zf", 32 * o, 32 * o + 32))
-        dma("s" if o == 0 else "a", "dy%d" % (4 + o), (T.y[:, 1024 + 128 * o:1152 + 128 * o],
-            T.yy[:, 1280 + 128 * o:1408 + 128 * o], YB(5, o)[1], []))
+        scatter(YB(4, o), LIST(4, 1), V("zf", 32 * o, 32 * o + 32))
+        dma("s" if o == 0 else "a", "dy%d" % (4 + o), (T.y[:, 1024 + 128 * o:1152 + 128 * o], YB(4, o)))
     for q in ("v", "a", "t", "g"):
         wait("g", csem[q], count[q])
     for s in sorted(ends):

@@ -1,4 +1,3 @@
-from concourse.bass import DstId, RemoteDMATransfer
 from concourse.mybir import dt, AluOpType, ActivationFunctionType
 
 P, K, R, O = 128, 32, 5, 2
@@ -14,24 +13,23 @@ def sb(kind, **widths):
 
 
 SCRATCH = {"ps": ("psum", [128, 4096], F4)}
-SCRATCH.update(sb(BF, cb=512, qb=20, wb=1024, rb=2560, ones=160, zeros=512, cm=160, cs=160, j3=[2, 32], pay=5, nz=2,
+SCRATCH.update(sb(BF, cb=512, qb=20, wb=1024, rb=2560, ones=160, zeros=128, cm=160, cs=160, j3=[2, 32], pay=5, nz=2,
                   oh0=[2, 64], oh1=[2, 64], ht0=[2, 128], ht1=[2, 128]))
 SCRATCH.update(sb(F4, onef=128, zerof=32, fd=128, fn=128, s0=256, f0=256, j33=33, ab=33, sg=33, col=4,
                   sq=640, kk=640, km=640, xa=320, uc=33, fa=64, dg=32, dc=32, ua=[4, 258], sn=96, uf=96,
-                  zl=256, zf=64, yy=1280))
+                  sp=256, zl=256, zf=64, yy=1280))
 SCRATCH.update(sb(I32, pi=1, pj=1))
-SCRATCH.update(sb(U16, dl=2, ls=2560))
-SCRATCH.update(sb(CODE, rq=640, wq=256, zq=128))
-SCRATCH.update(sb(PLANE, rs=640, ws=256))
+SCRATCH.update(sb(U16, dl=2, ls=2560, lin=2))
+SCRATCH.update(sb(CODE, rq=640, wq=256, pre=128))
+SCRATCH.update(sb(PLANE, rs=640, ws=256, prs=128))
 for _t in range(6):
-    _w = WW[_t] + (96 if _t else 0)
-    SCRATCH.update(sb(CODE, **{"win%d" % _t: _w}))
-    SCRATCH.update(sb(PLANE, **{"wis%d" % _t: _w}))
-for _t in range(5):
+    SCRATCH.update(sb(CODE, **{"win%d" % _t: WW[_t]}))
+    SCRATCH.update(sb(PLANE, **{"wis%d" % _t: WW[_t]}))
+for _t in range(1, 5):
     SCRATCH.update(sb(CODE, **{"out%d" % _t: 32}))
-    SCRATCH.update(sb(PLANE, **{"ous%d" % _t: 128}))
-DSEM = ["dc", "dq", "dw", "do"] + ["dn%d" % t for t in range(1, 6)] + ["dg%d" % t for t in range(2, 5)] + ["dy%d" % t for t in range(6)]
-SEMAPHORES = ["cv", "ca", "ct", "cg"] + DSEM + ["arr%d" % t for t in range(5)] + ["snd%d" % t for t in range(5)]
+    SCRATCH.update(sb(PLANE, **{"ous%d" % _t: 32}))
+DSEM = ["dc", "dq", "dw"] + ["dn%d" % t for t in range(1, 6)] + ["dg%d" % t for t in range(2, 5)] + ["dy%d" % t for t in range(6)]
+SEMAPHORES = ["cv", "ca", "ct", "cg"] + DSEM + ["arr%d" % t for t in range(6)] + ["snd%d" % t for t in range(6)]
 
 
 def rank_program(g, core, T, topo):
@@ -194,10 +192,9 @@ def rank_program(g, core, T, topo):
     iota(V("j3", 0, 32, half="all"), [[16, 2], [0, 2], [1, 16]])
     iota(V("pay", 0, 1), [[0, 1]], 1)
     iota(V("j33", 0, 33), [[1, 33]])
-    fill(V("zeros", 0, 512), 0.0)
+    fill(V("zeros", 0, 128), 0.0)
     fill(V("ones", 0, 160), 1.0)
     fill(V("s0", 0, 256, 2), 0.0)
-    quant("zq", "ous0", 0, 128, V("zeros", 0, 512))
     fill(V("zerof", 0, 32), 0.0)
     fill(V("ua", 192, 256, 2, half="all"), 0.0)
     fill(V("ua", 257, 258, half="all"), -TINY)
@@ -236,23 +233,23 @@ def rank_program(g, core, T, topo):
     def RANK(t):
         return V("cs", 159, 160) if t else V("cs", 127, 128)
 
-    def send(t):
+    def send(t, i, *moves):
         d = T.cores[rank ^ [1, 2, 4, 1, 2][t]]
         rid, pid = topo.addr(d, core)
-        es = topo.engines(core, d)[:8]
-        n = len(es) // 2
-        a = 128 + 32 * t if t < 4 else 128
-        waits("g", rg(V("out%d" % t, 0, 32), V("ous%d" % t, 0, 128)), [])
-        to = [DstId(rid=rid, pnc=pid)]
-        g.remote_dma_fused([
-            RemoteDMATransfer(dst_ids=to, dma_engine_mask=sum(1 << e for e in es[:n]), remote_sem=T.sem["arr%d" % t],
-                              srcs=[T["out%d" % t][:, 0:32].bitcast(dt.uint8)], dsts=[T["win%d" % (t + 1)][:, a:a + 32].bitcast(dt.uint8)]),
-            RemoteDMATransfer(dst_ids=to, dma_engine_mask=sum(1 << e for e in es[n:]), remote_sem=T.sem["arr%d" % t],
-                              srcs=[T["ous%d" % t][:, 0:128]], dsts=[T["wis%d" % (t + 1)][:, a:a + 128]])],
-            local_sem=T.sem["snd%d" % t])
-        ends["snd%d" % t] = ends["arr%d" % t] = 2 * n
-        wr.setdefault("win%d" % (t + 1), []).append((rg(V("win%d" % (t + 1), a, a + 32))[0], "x", "arr%d" % t, 2 * n))
-        wr.setdefault("wis%d" % (t + 1), []).append((rg(V("wis%d" % (t + 1), a, a + 128))[0], "x", "arr%d" % t, 2 * n))
+        n = len(topo.engines(core, d))
+        arr, snd = "arr%d" % i, "snd%d" % i
+        ends[snd] = ends[arr] = n * len(moves)
+        for (out, in_) in moves:
+            waits("g", in_[1], [])
+            g.remote_dma(out[0], in_[0], T.sem[arr], T.sem[snd], pid, rid, topo.mask(core, d))
+            wr.setdefault(out[1][0][0], []).append((out[1][0], "x", arr, ends[arr]))
+
+    def columns(q, s, a, qq, ss, b, n):
+        return ((AS(V(q, a, a + n), dt.uint8), AS(V(qq, b, b + n), dt.uint8)), (V(s, a, a + n), V(ss, b, b + n)))
+
+    def pick(q, s, a, qq, ss, n, off):
+        act(V(s, a, a + 32), IX(V(ss, 0, n), off), F.Copy)
+        cp(AS(V(q, a, a + 32), dt.uint32), IX(AS(V(qq, 0, n), dt.uint32), off))
 
     def mark(t, i):
         for c, h in ((0, LO), (32, HI)):
@@ -282,13 +279,13 @@ def rank_program(g, core, T, topo):
         turn(1) if t else gap()
         gather(t, 0, LO)
         gather(t, 0, HI)
-        gather(t, 1, LO) if t else gap()
-        w = WW[t]
-        act(V("ous%d" % t, 0, 32), IX(V("wis%d" % t, 0, w), LIST(t, 0)), F.Copy)
-        cp(AS(V("out%d" % t, 0, 32), dt.uint32), IX(AS(V("win%d" % t, 0, w), dt.uint32), LIST(t, 0)))
-        send(t)
         if t:
+            gather(t, 1, LO)
+            pick("out%d" % t, "ous%d" % t, 0, "win%d" % t, "wis%d" % t, WW[t], LIST(t, 0))
+            send(t, t, *columns("win%d" % (t + 1), "wis%d" % (t + 1), WW[t + 1] - 32, "out%d" % t, "ous%d" % t, 0, 32))
             gather(t, 1, HI)
+        else:
+            send(0, 0, (V("lin", 0, 2), LIST(0, 0)))
         gap(99)
 
     def signs(t):
@@ -309,13 +306,24 @@ def rank_program(g, core, T, topo):
             older(t, s)
             gap()
         scatter(row("km", t), lp, V("zerof", 0, 32))
-        act(V("dg", 0, 32), IX(row("km", t), V("dl", 0, 2)), F.Copy)
+        if t > 1:
+            diag(t)
         gap()
         tt(V("xa", 1, 256, 2), row("km", t), V("fn", 0, 128), A.mult)
-        tr(V("dc", 0, 32), V("dg", 0, 32))
+        if t > 1:
+            turned()
         gap()
-        ts(V("col", 2, 3), V("col", 1, 2), -5e18, A.mult, V("dc", 0, 1), A.subtract)
+        start()
         gap(99)
+
+    def diag(t):
+        act(V("dg", 0, 32), IX(row("km", t), V("dl", 0, 2)), F.Copy)
+
+    def turned():
+        tr(V("dc", 0, 32), V("dg", 0, 32))
+
+    def start():
+        ts(V("col", 2, 3), V("col", 1, 2), -5e18, A.mult, V("dc", 0, 1), A.subtract)
 
     def own(t):
         square(row("sq", t), mm("rq", "rs", 128 * t, "win0", "wis0", 0), 0, 128)
@@ -351,9 +359,15 @@ def rank_program(g, core, T, topo):
 
     def landed(t):
         w = ("win%d" % t, "wis%d" % t, 32 * t)
-        square(UA(t, 32 * t - 32, 32 * t), mm("rq", "rs", 128 * t, *w), 96, 128)
-        if t < 4:
+        if t == 1:
+            cp(UA(1, 0, 32), IX(V("sp", 0, 128), V("lin", 0, 2)))
+            act(V("sn", 0, 32), IX(V("sp", 128, 256), V("lin", 0, 2)), F.Copy)
+            pick("win1", "wis1", 128, "pre", "prs", 128, V("lin", 0, 2))
+        else:
+            square(UA(t, 32 * t - 32, 32 * t), mm("rq", "rs", 128 * t, *w), 96, 128)
+        if t in (2, 3):
             square(V("sn", 0, 32 * t), mm("rq", "rs", 128 * t + 128, *w), 128 - 32 * t, 128)
+        if t < 4:
             dma("s", "dg%d" % (t + 1), *move(t, t + 1, 128, 128 + 32 * t))
         if t in (2, 4):
             under_w(t, 32 * t, 64, 128, lambda o: V("zl", 128 * o + 32 * t - 64, 128 * o + 32 * t))
@@ -367,36 +381,35 @@ def rank_program(g, core, T, topo):
     rep(0, "v")
     quant("win0", "wis0", 0, 128, V("cb", 0, 512))
     quantq(0)
+    send(0, 5, *columns("pre", "prs", 0, "win0", "wis0", 0, 128))
     rep(1, "a")
     square(V("s0", 1, 256, 2), mm("rq", "rs", 0, "win0", "wis0", 0), 0, 128)
     b = mm("win0", "wis0", 0, "rq", "rs", 0)
     for t in range(1, 6):
         dma("s", "dn%d" % t, *move(0, t, 0, 128))
     dma("s", "dw", (V("wb", 0, 1024), T.w[:, 0:1024]))
-    dma("s", "do", *[(V("ous%d" % t, 32, 128), V("wis0", 32, 128)) for t in range(1, 5)])
+    rep(2, "v")
     quantq(1)
     own(1)
-    rep(2, "a")
+    quantq(2)
+    own(2)
+    rep(3, "a")
     ts(V("uc", 32, 33), PS(b, 0, 1), PS(b, 0, 1), A.mult, TINY, A.max)
     scan(V("xa", 0, 256), V("s0", 0, 256), V("f0", 0, 256), 0.0, A.max)
-    later()
-    later()
+    rep(4, "v")
     later((uses, 1))
-    later((floor, 1))
-    later((quantq, 2))
+    later((floor, 1), (diag, 1))
+    later((uses, 2))
+    later((floor, 2), (turned,))
     leave(0)
-    later()
-    later((own, 2), (rep, 3, "a"), (quant, "wq", "ws", 0, 256, V("wb", 0, 1024)))
+    for q in (1, 2):
+        later((lambda q: square(V("sp", 128 * q - 128, 128 * q), mm("rq", "rs", 128 * q, "pre", "prs", 0), 0, 128), q), (quantq, q + 2))
     ready(1)
-    uses(2)
-    quantq(3)
-    own(3)
-    under_w(0, 0, 0, 128, lambda o: YB(0, o))
-    floor(2)
     for t in range(1, 5):
         landed(t)
         if t == 1:
-            rep(4, "a")
+            own(3)
+            own(4)
         if t == 3:
             keep(0)
         if t == 4:
@@ -405,10 +418,10 @@ def rank_program(g, core, T, topo):
         leave(t)
         if t < 4:
             if t == 1:
-                quantq(4)
+                quant("wq", "ws", 0, 256, V("wb", 0, 1024))
             if t < 3:
                 later((uses, t + 2))
-                later((floor, t + 2), *([(own, 4)] if t == 1 else []))
+                later((floor, t + 2), *([(under_w, 0, 0, 0, 128, lambda o: YB(0, o))] if t == 1 else []))
             if t == 2:
                 later((lay, 0, 0))
                 later((lay, 0, 1))

@@ -1,8 +1,10 @@
+from concourse.bass import DstId, RemoteDMATransfer
 from concourse.mybir import dt, AluOpType, ActivationFunctionType
 
 P, K, R, O = 128, 32, 5, 2
 PREV = 1.0 - 2.0 ** -24
 TINY = 2.0 ** -121
+ROOT = 2.0 ** 63
 
 F4, BF, U16, I32, CODE, PLANE = "float32", "bfloat16", "uint16", "int32", "float8_e4m3fn_x4", "uint8"
 WW = [128, 160, 192, 224, 256, 160]
@@ -15,21 +17,22 @@ def sb(kind, **widths):
 SCRATCH = {"ps": ("psum", [128, 4096], F4)}
 SCRATCH.update(sb(BF, cb=512, qb=20, wb=1024, rb=2560, ones=160, zeros=128, cm=160, cs=160, j3=[2, 32], pay=5, nz=2,
                   oh0=[2, 64], oh1=[2, 64], ht0=[2, 128], ht1=[2, 128]))
-SCRATCH.update(sb(F4, onef=128, zerof=32, fd=128, fn=128, s0=256, f0=256, j33=33, ab=33, sg=33, col=4,
-                  sq=640, kk=640, km=640, xa=320, uc=33, fa=64, dg=32, dc=32, ua=[4, 258], sn=96, uf=96,
-                  sp=256, zl=256, zf=64, yy=1280))
+SCRATCH.update(sb(F4, onef=128, zerof=32, fd=128, fn=640, s0=256, f0=256, j33=33, ab=33, sg=33, col=5,
+                  sq=640, kk=640, km=640, xa=320, uc=33, fa=64, dg=32, dc=32, ua=[4, 258], sn=192, uf=192,
+                  sp=256, sx=224, pl=256, dd=[2, 32], dt=64, nb=64, nt=64, ni3=2, nc=64, zl=256, zf=64, yy=1280))
 SCRATCH.update(sb(I32, pi=1, pj=1))
-SCRATCH.update(sb(U16, dl=2, ls=2560, lin=2))
-SCRATCH.update(sb(CODE, rq=640, wq=256, pre=128))
-SCRATCH.update(sb(PLANE, rs=640, ws=256, prs=128))
+SCRATCH.update(sb(U16, dl=2, ls=2560, lin0=2, lin3=2, z8=8))
+SCRATCH.update(sb(CODE, rq=512, r4=128, wq=256, pre=128, pq=2, xq=128))
+SCRATCH.update(sb(PLANE, rs=512, s4=128, ws=256, prs=128, pqs=8, xs=128))
 for _t in range(6):
     SCRATCH.update(sb(CODE, **{"win%d" % _t: WW[_t]}))
     SCRATCH.update(sb(PLANE, **{"wis%d" % _t: WW[_t]}))
 for _t in range(1, 5):
     SCRATCH.update(sb(CODE, **{"out%d" % _t: 32}))
     SCRATCH.update(sb(PLANE, **{"ous%d" % _t: 32}))
-DSEM = ["dc", "dq", "dw"] + ["dn%d" % t for t in range(1, 6)] + ["dg%d" % t for t in range(2, 5)] + ["dy%d" % t for t in range(6)]
-SEMAPHORES = ["cv", "ca", "ct", "cg"] + DSEM + ["arr%d" % t for t in range(6)] + ["snd%d" % t for t in range(6)]
+DSEM = ["dc", "dq", "dw", "dp"] + ["dn%d" % t for t in range(1, 6)] + ["dg%d" % t for t in range(2, 5)] + ["dy%d" % t for t in range(6)]
+SENT = ["s0", "c0", "c1", "c2", "c3", "c4", "l0", "l1", "l3", "q2", "q4", "n1", "n3"]
+SEMAPHORES = ["cv", "ca", "ct", "cg"] + DSEM + ["arr" + s for s in SENT] + ["snd" + s for s in SENT]
 
 
 def rank_program(g, core, T, topo):
@@ -157,15 +160,15 @@ def rank_program(g, core, T, topo):
 
     bank = [0]
 
-    def mm(lq, ls, la, rq, rs, ra):
+    def mm(lq, ls, la, rq, rs, ra, n=128):
         b = 512 * (bank[0] % 8)
         bank[0] += 1
-        l, m, r, s = V(lq, la, la + 128), V(ls, la, la + 128), V(rq, ra, ra + 128), V(rs, ra, ra + 128)
-        op("t", lambda: g.tensor.matmul_mx(T.ps[:, b:b + 128], l[0], m[0], r[0], s[0], True, True), rg(l, m, r, s), rg(V("ps", b, b + 512)))
+        l, m, r, s = V(lq, la, la + 128), V(ls, la, la + 128), V(rq, ra, ra + n), V(rs, ra, ra + n)
+        op("t", lambda: g.tensor.matmul_mx(T.ps[:, b:b + n], l[0], m[0], r[0], s[0], True, True), rg(l, m, r, s), rg(V("ps", b, b + 512)))
         return b
 
-    def PS(b, lo, hi):
-        return (T.ps[:, b + lo:b + hi], rg(V("ps", b, b + 512)))
+    def PS(b, lo, hi, part=ALL):
+        return (V("ps", b + lo, b + hi, part=part)[0], rg(V("ps", b, b + 512)))
 
     def iota(v, pattern, cm=0):
         if v[1][0][0] == "pi":
@@ -173,15 +176,9 @@ def rank_program(g, core, T, topo):
         else:
             op("g", lambda: g.iota(v[0], pattern, 0, cm, allow_small_or_imprecise_dtypes=True), [], v[1])
 
-    fillers = []
-
-    def later(*calls):
-        fillers.append(calls)
-
-    def gap(k=1):
-        for _ in range(k):
-            for c in (fillers.pop(0) if fillers else ()):
-                c[0](*c[1:])
+    def do(calls):
+        for c in calls:
+            c[0](*c[1:])
 
     dma("a", "dq", (V("qb", 0, 20), T.qt[:, 0:20]))
     dma("s", "dc", (V("cb", 0, 512), T.c[:, 0:512]))
@@ -189,13 +186,15 @@ def rank_program(g, core, T, topo):
     fill(ONE, 1.0)
     iota(V("pi", 0, 1), [[0, 1]], 1)
     op("g", lambda: g.affine_select(T.fd[:, 0:128], ONE[0], [[1, 128]], A.is_ge, PREV, 0, -1), ONE[1], rg(V("fd", 0, 128)))
-    iota(V("j3", 0, 32, half="all"), [[16, 2], [0, 2], [1, 16]])
-    iota(V("pay", 0, 1), [[0, 1]], 1)
     iota(V("j33", 0, 33), [[1, 33]])
+    iota(V("pay", 0, 1), [[0, 1]], 1)
+    iota(V("j3", 0, 32, half="all"), [[16, 2], [0, 2], [1, 16]])
+    iota(V("pl", 0, 128), [[1, 128]])
     fill(V("zeros", 0, 128), 0.0)
     fill(V("ones", 0, 160), 1.0)
     fill(V("s0", 0, 256, 2), 0.0)
     fill(V("zerof", 0, 32), 0.0)
+    fill(V("z8", 0, 8), 0)
     fill(V("ua", 192, 256, 2, half="all"), 0.0)
     fill(V("ua", 257, 258, half="all"), -TINY)
     ts(V("pj", 0, 1), V("pi", 0, 1), 128 - 1 - 16, A.bitwise_and)
@@ -203,11 +202,16 @@ def rank_program(g, core, T, topo):
     ts(V("f0", 1, 256, 2), V("fd", 0, 128), TINY, A.mult)
     for c in range(2):
         ts(V("dl", c, c + 1), V("pj", 0, 1), 16.0 * c, A.add)
-    act(V("fn", 0, 128), V("fd", 0, 128), F.Copy, scale=-1.0)
-    fill(V("j33", 32, 33), 31.5)
+    def steps(*ts):
+        for t in ts:
+            act(V("fn", 128 * t, 128 * t + 128), V("fd", 0, 128), F.Copy, scale=-1.0)
 
-    def rep(t, on):
-        for e in range(4):
+    steps(0, 1, 2)
+    ts(V("j33", 0, 32), V("j33", 0, 32), -0.5, A.add)
+    fill(V("j33", 32, 33), 31.0)
+
+    def rep(t, on, es=range(4)):
+        for e in es:
             o, q = (T.rb[:, 512 * t + e:512 * t + 512:4], [("rb%d" % e, t, t + 1, 0, 128, None)]), V("qb", 4 * t + e, 4 * t + e + 1)
             if on == "v":
                 ts(o, V("ones", 0, 128), q, A.mult)
@@ -215,7 +219,7 @@ def rank_program(g, core, T, topo):
                 act(o, V("zeros", 0, 128), F.Identity, bias=q)
 
     def quantq(t):
-        quant("rq", "rs", 128 * t, 128 * t + 128, (T.rb[:, 512 * t:512 * t + 512], [("rb%d" % e, t, t + 1, 0, 128, None) for e in range(4)]))
+        quant(*(("rq", "rs", 128 * t, 128 * t + 128) if t < 4 else ("r4", "s4", 0, 128)), (T.rb[:, 512 * t:512 * t + 512], [("rb%d" % e, t, t + 1, 0, 128, None) for e in range(4)]))
 
     def square(dst, b, lo, hi):
         act(dst, PS(b, lo, hi), F.Square)
@@ -236,28 +240,37 @@ def rank_program(g, core, T, topo):
     def send(t, i, *moves):
         d = T.cores[rank ^ [1, 2, 4, 1, 2][t]]
         rid, pid = topo.addr(d, core)
-        n = len(topo.engines(core, d))
-        arr, snd = "arr%d" % i, "snd%d" % i
-        ends[snd] = ends[arr] = n * len(moves)
+        es = topo.engines(core, d)
+        arr, snd = "arr" + i, "snd" + i
+        if i[0] == "q":
+            n = len(es) // 2
+            waits("g", rg(moves[0][1], moves[1][1]), [])
+            g.remote_dma_fused([RemoteDMATransfer(dst_ids=[DstId(rid=rid, pnc=pid)], dma_engine_mask=sum(1 << e for e in s), remote_sem=T.sem[arr],
+                                                  srcs=[in_[0]], dsts=[out[0]]) for (out, in_), s in zip(moves, (es[:n], es[n:]))], local_sem=T.sem[snd])
+            ends[snd] = ends[arr] = 2 * n
+            for (out, in_) in moves:
+                wr.setdefault(out[1][0][0], []).append((out[1][0], "x", arr, ends[arr]))
+            return
+        ends[snd] = ends[arr] = len(es) * len(moves)
         for (out, in_) in moves:
             waits("g", in_[1], [])
-            g.remote_dma(out[0], in_[0], T.sem[arr], T.sem[snd], pid, rid, topo.mask(core, d))
+            g.remote_dma(out[0], in_[0], T.sem[arr], T.sem[snd], pid, rid, sum(1 << e for e in es))
             wr.setdefault(out[1][0][0], []).append((out[1][0], "x", arr, ends[arr]))
 
     def columns(q, s, a, qq, ss, b, n):
         return ((AS(V(q, a, a + n), dt.uint8), AS(V(qq, b, b + n), dt.uint8)), (V(s, a, a + n), V(ss, b, b + n)))
 
-    def pick(q, s, a, qq, ss, n, off):
-        act(V(s, a, a + 32), IX(V(ss, 0, n), off), F.Copy)
-        cp(AS(V(q, a, a + 32), dt.uint32), IX(AS(V(qq, 0, n), dt.uint32), off))
+    def pick(q, s, a, qq, ss, n, off, k=32):
+        act(V(s, a, a + k), IX(V(ss, 0, n), off), F.Copy)
+        cp(AS(V(q, a, a + k), dt.uint32), IX(AS(V(qq, 0, n), dt.uint32), off))
 
     def mark(t, i):
         for c, h in ((0, LO), (32, HI)):
             ts(V("oh%d" % i, c, c + 32, part=LO, half="all"), V("j3", 0, 32, part=h, half="all"), V("cs", RANK(t)[1][0][1], RANK(t)[1][0][2], part=h),
                A.is_equal, V("pay", 0 if i else t, 1 if i else t + 1, part=h), A.mult)
 
-    def turn(i):
-        for c, to, h in ((0, LO, LO), (64, B1, B0), (64, B0, B1)):
+    def turn(i, a=0, b=3):
+        for c, to, h in ((0, LO, LO), (64, B1, B0), (64, B0, B1))[a:b]:
             tr(V("ht%d" % i, c, c + 64, part=to, half="all"), V("oh%d" % i, 0, 64, part=h, half="all"))
 
     def gather(t, i, h):
@@ -265,56 +278,53 @@ def rank_program(g, core, T, topo):
         for j in range(2):
             scan(V("ls", a + j, a + 256, 2, part=h), V("ones", 0, 128, part=LO), V("ht%d" % i, 0, 128, part=LO, half=j), 0.0, A.max)
 
-    def leave(t):
+    def leave(t, *between):
         n = 160 if t else 128
         ts(V("cm", 0, n), V("xa", 1, 2 * n, 2), V("uc", 32, 33), A.is_gt if t else A.is_lt)
-        gap()
+        do(between[0])
         scan(V("cs", 0, n), V("ones", 0, n), V("cm", 0, n), -32.0 if t else 0.0, A.add)
-        gap()
-        mark(t, 0)
+        do(between[1])
+        i = 0
+        mark(t, i)
         if t < 4:
             signs(t)
-        mark(t, 1) if t else gap()
-        turn(0)
-        turn(1) if t else gap()
-        gather(t, 0, LO)
-        gather(t, 0, HI)
-        if t:
-            gather(t, 1, LO)
-            pick("out%d" % t, "ous%d" % t, 0, "win%d" % t, "wis%d" % t, WW[t], LIST(t, 0))
-            send(t, t, *columns("win%d" % (t + 1), "wis%d" % (t + 1), WW[t + 1] - 32, "out%d" % t, "ous%d" % t, 0, 32))
-            gather(t, 1, HI)
-        else:
-            send(0, 0, (V("lin", 0, 2), LIST(0, 0)))
-        gap(99)
+        do(between[2])
+        if t == 3:
+            newslot(t)
+        turn(i)
+        if t == 0:
+            newslot(t)
+        do(between[3])
+        gather(t, i, LO)
+        gather(t, i, HI)
+        if t in (0, 3):
+            send(t, "l%d" % t, (V("lin%d" % t, 0, 2), LIST(t, i)))
+        do(between[4])
+        if t in (1, 2, 4):
+            hand(t)
+
+    def hand(t):
+        pick("out%d" % t, "ous%d" % t, 0, "win%d" % t, "wis%d" % t, WW[t], LIST(t, 0))
+        send(t, "c%d" % t, *columns("win%d" % (t + 1), "wis%d" % (t + 1), WW[t + 1] - 32, "out%d" % t, "ous%d" % t, 0, 32))
+
+    def slots(t):
+        ts(V("pay", t, t + 1), V("nz", 0, 1), V("nz", 1, 2), A.min, V("pay", t - 1, t), A.max)
+
+    def newslot(t):
+        ts(V("nz", 0, 1), RANK(t), 128.0 + 32 * t, A.add)
 
     def signs(t):
-        r = RANK(t)
-        act(V("col", 0, 1), r, F.Identity, scale=-1.0, bias=-0.5)
-        act(V("nz", 0, 1), r, F.Identity, bias=128.0 + 32 * t)
-        act(V("ab", 0, 33), V("j33", 0, 33), F.Abs, bias=V("col", 0, 1))
-        act(V("nz", 1, 2), r, F.Identity, scale=-1000.0, bias=32000.0)
+        act(V("ab", 0, 33), V("j33", 0, 33), F.Abs, scale=-1.0, bias=RANK(t))
+        act(V("nz", 1, 2), RANK(t), F.Relu, scale=-ROOT / 16, bias=31.5 * ROOT / 16)
         act(V("sg", 0, 33), V("ab", 0, 33), F.Sign, bias=-0.75)
-        act(V("col", 1, 2), r, F.Relu, scale=-1e18, bias=31.5e18)
 
-    def ready(t):
+    def ready(t, between=()):
         lp = LIST(t - 1, 1)
         act(V("fa", 0, 64, 2), IX(V("fn", 0, 128), lp), F.Copy)
         act(V("fa", 1, 64, 2), IX(V("fn", 0, 128), lp), F.Copy, scale=TINY)
-        ts(V("pay", t, t + 1), V("nz", 0, 1), V("nz", 1, 2), A.min, V("pay", t - 1, t), A.max)
-        for s in range(1, t - 1):
-            older(t, s)
-            gap()
-        scatter(row("km", t), lp, V("zerof", 0, 32))
-        if t > 1:
-            diag(t)
-        gap()
-        tt(V("xa", 1, 256, 2), row("km", t), V("fn", 0, 128), A.mult)
-        if t > 1:
-            turned()
-        gap()
-        start()
-        gap(99)
+        scatter(row("fn", t), lp, V("zerof", 0, 32))
+        do(between)
+        tt(V("xa", 1, 256, 2), row("km", t), row("fn", t), A.mult)
 
     def diag(t):
         act(V("dg", 0, 32), IX(row("km", t), V("dl", 0, 2)), F.Copy)
@@ -323,13 +333,14 @@ def rank_program(g, core, T, topo):
         tr(V("dc", 0, 32), V("dg", 0, 32))
 
     def start():
-        ts(V("col", 2, 3), V("col", 1, 2), -5e18, A.mult, V("dc", 0, 1), A.subtract)
+        ts(V("col", 2, 3), V("nz", 1, 2), -ROOT, A.mult, V("dc", 0, 1), A.subtract)
 
     def own(t):
         square(row("sq", t), mm("rq", "rs", 128 * t, "win0", "wis0", 0), 0, 128)
 
-    def uses(t):
-        tt(row("kk", t), row("kk", t - 1) if t > 1 else V("s0", 1, 256, 2), row("sq", t), A.add)
+    def uses(t, a, b):
+        c = 128 * t
+        tt(V("kk", c + a, c + b), V("kk", c - 128 + a, c - 128 + b) if t > 1 else V("s0", 2 * a + 1, 2 * b, 2), V("sq", c + a, c + b), A.add)
 
     def floor(t):
         ts(row("km", t), row("kk", t), TINY, A.max)
@@ -341,103 +352,195 @@ def rank_program(g, core, T, topo):
     def YB(t, o):
         return V("yy", 256 * t + 128 * o, 256 * t + 128 * o + 128)
 
-    def under_w(win, a, lo, hi, dst):
-        for o in range(O):
-            b = mm("wq", "ws", 128 * o, "win%d" % win, "wis%d" % win, a)
-            act(dst(o), PS(b, lo, hi), F.Copy)
+    def under_w(t, os=range(O)):
+        for o in os:
+            a, n = (0, 192) if t == 2 else (128, 128)
+            b = mm("wq", "ws", 128 * o, "win%d" % t, "wis%d" % t, a, n)
+            act(V("zl", 128 * o + 32 * t - 64, 128 * o + 32 * t), PS(b, n - 64, n), F.Copy)
+            if t == 2:
+                act(YB(0, o), PS(b, 0, 128), F.Copy)
+
+    def UF(t, a, b):
+        return V("uf", 96 * (t % 2) + a, 96 * (t % 2) + b)
+
+    def SN(t, a, b):
+        return V("sn", 96 * (t % 2) + a, 96 * (t % 2) + b)
+
+    def more(t, a, b):
+        tt(UA(t, a, b), UA(t - 1, a, b), SN(t, a, b), A.add)
+
+    def raised(t, a, b):
+        ts(UF(t, a, b), UA(t, a, b), TINY, A.max)
+
+    def spread(j):
+        act(V("nc", 32 * j, 32 * j + 32), V("zerof", 0, 32), F.Identity, bias=V("ni3", j, j + 1))
 
     def lay(t, o):
         scatter(YB(t, o), LIST(t, 1), V("zl", 128 * o + 32 * t, 128 * o + 32 * t + 32))
 
-    def keep(t):
-        for o in range(O):
-            act(YB(t + 1, o), YB(t, o), F.Copy)
-        dma("s", "dy%d" % t, (T.y[:, 256 * t:256 * t + 256], V("yy", 256 * t, 256 * t + 256)))
+    def keep(t, o):
+        act(YB(t + 1, o), YB(t, o), F.Copy)
+        if o == 1:
+            dma("s", "dy%d" % t, (T.y[:, 256 * t:256 * t + 256], V("yy", 256 * t, 256 * t + 256)))
 
     def older(t, s):
-        scatter(row("km", t), LIST(s, 1), V("uf", 32 * s, 32 * s + 32))
+        scatter(row("km", t), LIST(s, 1), UF(t, 32 * s, 32 * s + 32))
 
     def landed(t):
         w = ("win%d" % t, "wis%d" % t, 32 * t)
         if t == 1:
-            cp(UA(1, 0, 32), IX(V("sp", 0, 128), V("lin", 0, 2)))
-            act(V("sn", 0, 32), IX(V("sp", 128, 256), V("lin", 0, 2)), F.Copy)
-            pick("win1", "wis1", 128, "pre", "prs", 128, V("lin", 0, 2))
-        else:
-            square(UA(t, 32 * t - 32, 32 * t), mm("rq", "rs", 128 * t, *w), 96, 128)
-        if t in (2, 3):
-            square(V("sn", 0, 32 * t), mm("rq", "rs", 128 * t + 128, *w), 128 - 32 * t, 128)
-        if t < 4:
-            dma("s", "dg%d" % (t + 1), *move(t, t + 1, 128, 128 + 32 * t))
-        if t in (2, 4):
-            under_w(t, 32 * t, 64, 128, lambda o: V("zl", 128 * o + 32 * t - 64, 128 * o + 32 * t))
+            cp(UA(1, 0, 32), IX(V("sp", 0, 128), V("lin0", 0, 2)))
+            act(SN(2, 0, 32), IX(V("sp", 128, 256), V("lin0", 0, 2)), F.Copy)
+            pick("win1", "wis1", 128, "pre", "prs", 128, V("lin0", 0, 2))
+        elif t == 2:
+            square(UA(2, 32, 64), mm("rq", "rs", 256, *w), 96, 128)
+            square(SN(3, 0, 64), mm("rq", "rs", 384, *w), 64, 128)
+            b = mm("r4", "s4", 0, "win2", "wis2", 0, 192)
+            square(row("sq", 4), b, 0, 128)
+            square(SN(4, 0, 64), b, 128, 192)
+            under_w(2)
+        elif t == 3:
+            square(UA(3, 64, 96), mm("rq", "rs", 384, *w), 96, 128)
+            square(SN(4, 64, 96), mm("r4", "s4", 0, *w), 96, 128)
+            square(V("nb", 0, 64), mm("xq", "xs", 0, *w), 64, 128)
         scan(V("uc", 0, 33), V("sg", 0, 33), V("ua", 193, 258, 2, half=t - 1), V("col", 2, 3), A.min)
         scan(V("xa", 256, 320), V("ua", 192, 256, half=t - 1), V("fa", 0, 64), 0.0, A.min)
+        if t == 1:
+            wait("s", "arrl0", ends["arrl0"])
+            dma("s", "dn2", *move(0, 2, 0, 128))
         if t < 4:
-            tt(UA(t + 1, 0, 32 * t), UA(t, 0, 32 * t), V("sn", 0, 32 * t), A.add)
-            later((ts, V("uf", 0, 32 * t), UA(t + 1, 0, 32 * t), TINY, A.max))
-            later((older, t + 1, 0))
+            dma("s", "dg%d" % (t + 1), *move(t, t + 1, 128, 128 + 32 * t))
+            dma("s", "dn%d" % (t + 2), *move(0, t + 2, 0 if t < 3 else 32, 128))
+
+    def query(q, s, b, qq, ss, a):
+        return (AS(V(q, b, b + 2), dt.uint8), AS(V(qq, a, a + 2), dt.uint8)), (V(s, b, b + 8), V(ss, a, a + 8))
 
     rep(0, "v")
     quant("win0", "wis0", 0, 128, V("cb", 0, 512))
     quantq(0)
-    send(0, 5, *columns("pre", "prs", 0, "win0", "wis0", 0, 128))
+    send(0, "c0", *columns("pre", "prs", 0, "win0", "wis0", 0, 128))
     rep(1, "a")
+    rep(4, "a", (0, 1))
     square(V("s0", 1, 256, 2), mm("rq", "rs", 0, "win0", "wis0", 0), 0, 128)
     b = mm("win0", "wis0", 0, "rq", "rs", 0)
-    for t in range(1, 6):
-        dma("s", "dn%d" % t, *move(0, t, 0, 128))
+    dma("s", "dn1", *move(0, 1, 0, 128))
     dma("s", "dw", (V("wb", 0, 1024), T.w[:, 0:1024]))
     rep(2, "v")
     quantq(1)
     own(1)
     quantq(2)
     own(2)
-    rep(3, "a")
+    rep(4, "a", (2, 3))
+    rep(3, "v")
     ts(V("uc", 32, 33), PS(b, 0, 1), PS(b, 0, 1), A.mult, TINY, A.max)
     scan(V("xa", 0, 256), V("s0", 0, 256), V("f0", 0, 256), 0.0, A.max)
-    rep(4, "v")
-    later((uses, 1))
-    later((floor, 1), (diag, 1))
-    later((uses, 2))
-    later((floor, 2), (turned,))
-    leave(0)
+    quantq(3)
+    leave(0, [(uses, 1, 0, 64)], [(uses, 1, 64, 128)], [(quantq, 4)], [(floor, 1), (diag, 1)],
+          [(slots, 1), (turned,)])
+    send(3, "q4", *query("pq", "pqs", 0, "r4", "s4", 0))
     for q in (1, 2):
-        later((lambda q: square(V("sp", 128 * q - 128, 128 * q), mm("rq", "rs", 128 * q, "pre", "prs", 0), 0, 128), q), (quantq, q + 2))
-    ready(1)
-    for t in range(1, 5):
-        landed(t)
-        if t == 1:
-            own(3)
-            own(4)
-        if t == 3:
-            keep(0)
-        if t == 4:
-            later((lay, 1, 0))
-            later((lay, 1, 1), (keep, 1))
-        leave(t)
-        if t < 4:
-            if t == 1:
-                quant("wq", "ws", 0, 256, V("wb", 0, 1024))
-            if t < 3:
-                later((uses, t + 2))
-                later((floor, t + 2), *([(under_w, 0, 0, 0, 128, lambda o: YB(0, o))] if t == 1 else []))
-            if t == 2:
-                later((lay, 0, 0))
-                later((lay, 0, 1))
-            ready(t + 1)
-    for t in (2, 3):
-        lay(t, 0)
-        lay(t, 1)
-        keep(t)
+        square(V("sp", 128 * q - 128, 128 * q), mm("rq", "rs", 128 * q, "pre", "prs", 0), 0, 128)
+    ready(1, [(start,), (uses, 2, 0, 64)])
+    def second(t, *more_calls):
+        return [(mark, t, 1)], [(turn, 1)], [(gather, t, 1, LO)] + list(more_calls)
+
+    def BLOCK(d):
+        return (32 * d, 32 * d + 32)
+
+    def quantw(o):
+        quant("wq", "ws", 128 * o, 128 * o + 128, V("wb", 512 * o, 512 * o + 512))
+
+    def where(t):
+        act(V("pl", 128 + 32 * t, 160 + 32 * t), IX(V("pl", 0, 128 + 32 * t), LIST(t, 0)), F.Copy)
+
+    def twice(t):
+        for j in range(2):
+            act(V("dd", 0, 32, half=j), IX(V("pl", 0, 128 + 32 * t), LIST(t, 0)), F.Copy)
+
+    def across():
+        for c in range(2):
+            tr(V("dt", 32 * c, 32 * c + 32), V("dd", 16 * c, 16 * c + 16, half="all"))
+
+    def listed(t):
+        cp(LIST(t, 1), V("dt", 0, 64, 32))
+
+    landed(1)
+    where(0)
+    own(3)
+    square(V("sx", 0, 128), mm("r4", "s4", 0, "pre", "prs", 0), 0, 128)
+    steps(3, 4)
+    uses(2, 64, 128)
+    leave(1, [(more, 2, 0, 32)], [(floor, 2), (raised, 2, 0, 32)], [(uses, 3, 0, 64)], [(older, 2, 0), (diag, 2)], [(newslot, 1)])
+    twice(1)
+    where(1)
+    turned()
+    uses(3, 64, 128)
+    slots(2)
+    start()
+    across()
+    floor(3)
+    listed(1)
+    quantw(0)
+    ready(2, [(quantw, 1)])
+    pick("xq", "xs", 0, "pq", "pqs", 2, V("z8", 0, 8), 128)
+
+    landed(2)
+    leave(2, [(more, 3, 0, 64)], [(raised, 3, 0, 64), (uses, 4, 0, 64)], [(uses, 4, 64, 128)], [(older, 3, 0)], [(newslot, 2)])
+    older(3, 1)
+    twice(2)
+    diag(3)
+    where(2)
+    more(4, 0, 64)
+    across()
+    floor(4)
+    slots(3)
+    listed(2)
+    raised(4, 0, 64)
+    turned()
+    ready(3, [(older, 4, 0), (start,)])
+    older(4, 1)
+    act(V("sx", 128, 160), IX(row("sq", 4), LIST(0, 0)), F.Copy)
+    lay(0, 0)
+
+    landed(3)
+    more(4, 64, 96)
+    a, b, c = second(3, (gather, 3, 1, HI))
+    leave(3, [(raised, 4, 64, 96), (tr, V("nt", 0, 64, 2), V("nb", 0, 32)), (tr, V("nt", 1, 64, 2), V("nb", 32, 64)),
+              (send, 3, "n3", (V("ni3", 0, 2), V("nt", 0, 2)))], [(older, 4, 2)], a + [(diag, 4), (spread, 0), (spread, 1)], b, c + [(turned,)])
+    hand(3)
+    ready(4, [(start,), (slots, 4), (tr, V("sx", 160, 224), V("nc", 0, 64))])
+    cp(UA(4, 96, 128), IX(V("sx", 0, 224), V("lin3", 0, 2)))
+
+    keep(0, 0)
+    where(3)
+    landed(4)
+    lay(0, 1)
+    keep(0, 1)
+    leave(4, [(lay, 1, 0), (keep, 1, 0)], [], [], [(lay, 1, 1), (keep, 1, 1)], [])
+    under_w(4)
+    lay(2, 0)
+    keep(2, 0)
+    lay(2, 1)
+    keep(2, 1)
+    twice(4)
+    lay(3, 0)
+    keep(3, 0)
+    lay(3, 1)
+    wait("s", "sndc4", ends["sndc4"])
+    keep(3, 1)
+    across()
+    listed(4)
 
     bs = [mm("wq", "ws", 128 * o, "win5", "wis5", 32) for o in range(O)]
-    cp(V("zf", 0, 32), PS(bs[0], 96, 128))
-    act(V("zf", 32, 64), PS(bs[1], 96, 128), F.Copy)
+    for o in range(O):
+        cp(V("zf", 32 * o, 32 * o + 32), PS(bs[o], 96, 128))
     for o in range(O):
         scatter(YB(4, o), LIST(4, 1), V("zf", 32 * o, 32 * o + 32))
         dma("s" if o == 0 else "a", "dy%d" % (4 + o), (T.y[:, 1024 + 128 * o:1152 + 128 * o], YB(4, o)))
-    for q in ("v", "a", "t", "g"):
-        wait("g", csem[q], count[q])
     for s in sorted(ends):
-        wait("g", s, ends[s])
+        if s not in ("dy4", "dy5"):
+            wait("g", s, ends[s])
+    for q in ("g", "t", "a", "v"):
+        wait("g", csem[q], count[q])
+    wait("s", "dy4", ends["dy4"])
+    wait("a", "dy5", ends["dy5"])

from concourse.bass import DstId, RemoteDMATransfer
from concourse.mybir import dt, AluOpType, ActivationFunctionType

P, K, R, O = 128, 32, 5, 2
PREV = 1.0 - 2.0 ** -24
TINY = 2.0 ** -121
ROOT = 2.0 ** 63

F4, BF, U16, I32, CODE, PLANE = "float32", "bfloat16", "uint16", "int32", "float8_e4m3fn_x4", "uint8"
WW = [128, 160, 192, 224, 256, 160]


def sb(kind, **widths):
    return {n: ("sbuf", [128] + (w if isinstance(w, list) else [w]), kind) for n, w in widths.items()}


SCRATCH = {"ps": ("psum", [128, 4096], F4)}
SCRATCH.update(sb(BF, cb=512, qb=20, wb=1024, rb=2560, ones=160, zeros=128, cm=160, cs=160, j3=[2, 32], pay=5, nz=2,
                  oh0=[2, 64], oh1=[2, 64], ht0=[2, 128], ht1=[2, 128]))
SCRATCH.update(sb(F4, onef=128, zerof=32, fd=128, fn=640, s0=256, f0=256, j33=33, ab=33, sg=33, col=5,
                  sq=640, kk=640, km=640, xa=320, uc=33, fa=64, dg=32, dc=32, ua=[4, 258], sn=192, uf=192,
                  sp=256, sx=224, pl=256, dd=[2, 32], dt=64, nb=64, nt=64, ni3=2, nc=64, zl=256, zf=64, yy=1280))
SCRATCH.update(sb(I32, pi=1, pj=1))
SCRATCH.update(sb(U16, dl=2, ls=2560, lin0=2, lin3=2, z8=8))
SCRATCH.update(sb(CODE, rq=512, r4=128, wq=256, pre=128, pq=2, xq=128))
SCRATCH.update(sb(PLANE, rs=512, s4=128, ws=256, prs=128, pqs=8, xs=128))
for _t in range(6):
    SCRATCH.update(sb(CODE, **{"win%d" % _t: WW[_t]}))
    SCRATCH.update(sb(PLANE, **{"wis%d" % _t: WW[_t]}))
for _t in range(1, 5):
    SCRATCH.update(sb(CODE, **{"out%d" % _t: 32}))
    SCRATCH.update(sb(PLANE, **{"ous%d" % _t: 32}))
DSEM = ["dc", "dq", "dw", "dp"] + ["dn%d" % t for t in range(1, 6)] + ["dg%d" % t for t in range(2, 5)] + ["dy%d" % t for t in range(6)]
SENT = ["s0", "c0", "c1", "c2", "c3", "c4", "l0", "l1", "l3", "q2", "q4", "n1", "n3"]
SEMAPHORES = ["cv", "ca", "ct", "cg"] + DSEM + ["arr" + s for s in SENT] + ["snd" + s for s in SENT]


def rank_program(g, core, T, topo):
    rank = T.rank_of(core)
    if rank is None:
        return
    A, F = AluOpType, ActivationFunctionType
    eng = {"v": g.vector, "a": g.scalar, "t": g.tensor, "g": g, "s": g.sync}
    csem = {"v": "cv", "a": "ca", "t": "ct", "g": "cg"}
    count = {"v": 0, "a": 0, "t": 0, "g": 0}
    known = {q: {} for q in eng}
    snap = {}
    wr, rd = {}, {}
    ends = {}

    def wait(q, sem, val):
        if known[q].get(sem, 0) >= val:
            return
        eng[q].wait_ge(T.sem[sem], val)
        known[q][sem] = val
        for s, v in snap.get((sem, val), {}).items():
            if known[q].get(s, 0) < v:
                known[q][s] = v

    def meet(x, y):
        return x[1] < y[2] and y[1] < x[2] and x[3] < y[4] and y[3] < x[4] and (x[5] == y[5] or None in (x[5], y[5]))

    def inside(x, y):
        return y[1] <= x[1] and x[2] <= y[2] and y[3] <= x[3] and x[4] <= y[4] and y[5] in (None, x[5])

    def waits(q, reads, writes):
        need = {}
        for x in reads + writes:
            for (y, q2, s, v) in wr.get(x[0], ()):
                if meet(x, y):
                    need[s] = max(need.get(s, 0), v)
        for x in writes:
            for (y, q2, s, v) in rd.get(x[0], ()):
                if meet(x, y) and (q2 != q or s[0] == "d"):
                    need[s] = max(need.get(s, 0), v)
        for s in sorted(need):
            wait(q, s, need[s])

    def note(q, reads, writes, sem, val):
        snap[(sem, val)] = dict(known[q])
        for x in writes:
            wr[x[0]] = [e for e in wr.get(x[0], ()) if not inside(e[0], x)] + [(x, q, sem, val)]
            rd[x[0]] = [e for e in rd.get(x[0], ()) if not inside(e[0], x)]
        for x in reads:
            rd.setdefault(x[0], []).append((x, q, sem, val))

    def op(q, fn, reads, writes):
        waits(q, reads, writes)
        ins = fn()
        count[q] += 1
        ins.then_inc(T.sem[csem[q]], 1)
        note(q, reads, writes, csem[q], count[q])

    def dma(q, sem, *moves):
        for (out, in_) in moves:
            waits(q, rg(in_), rg(out))
            eng[q].dma_start(ap(out), ap(in_)).then_inc(T.sem[sem], 16)
        ends[sem] = 16 * len(moves)
        for (out, in_) in moves:
            note(q, rg(in_), rg(out), sem, ends[sem])

    ALL, LO, HI, B0, B1 = (0, 128), (0, 64), (64, 128), (0, 32), (32, 64)

    def V(n, a, b, step=1, part=ALL, half=None):
        cols = slice(a, b) if step == 1 else slice(a, b, step)
        rows = slice(None) if part == ALL else slice(part[0], part[1])
        odd = a % 2 if step == 2 else None
        if half is None:
            return (T[n][rows, cols], [(n, a, b, part[0], part[1], odd)])
        if half == "all":
            return (T[n][rows, :, cols], [(n + "/%d" % j, a, b, part[0], part[1], odd) for j in range(T[n].shape[1])])
        return (T[n][rows, half, cols], [(n + "/%d" % half, a, b, part[0], part[1], odd)])

    def IX(v, off):
        return (v[0].indirect(off[0]), v[1] + off[1])

    def AS(v, d):
        return (v[0].bitcast(d), v[1])

    def ap(x):
        return x[0] if isinstance(x, tuple) else x

    def rg(*xs):
        r = []
        for x in xs:
            if isinstance(x, tuple):
                r += x[1]
        return r

    def ts(out, i0, s1, op0, s2=None, op1=None):
        if op1 is None:
            op("v", lambda: g.vector.tensor_scalar(ap(out), ap(i0), ap(s1), None, op0), rg(i0, s1), rg(out))
        else:
            op("v", lambda: g.vector.tensor_scalar(ap(out), ap(i0), ap(s1), ap(s2), op0, op1), rg(i0, s1, s2), rg(out))

    def tt(out, i0, i1, o):
        op("v", lambda: g.vector.tensor_tensor(ap(out), ap(i0), ap(i1), o), rg(i0, i1), rg(out))

    def cp(out, in_):
        op("v", lambda: g.vector.tensor_copy(ap(out), ap(in_)), rg(in_), rg(out))

    def scatter(win, off, vals):
        op("v", lambda: g.vector.tensor_copy(win[0].indirect(off[0]), ap(vals)), rg(off, vals), rg(win))

    def tr(out, in_):
        op("v", lambda: g.vector.transpose(ap(out), ap(in_)), rg(in_), rg(out))

    def scan(out, d0, d1, start, o):
        op("v", lambda: g.vector.tensor_tensor_scan(ap(out), ap(d0), ap(d1), ap(start), A.mult, o), rg(d0, d1, start), rg(out))

    def fill(v, c):
        op("v", lambda: g.vector.memset(ap(v), c), [], rg(v))

    def quant(q, s, a, b, in_):
        x, y = V(q, a, b), V(s, a, b)
        op("v", lambda: g.vector.quantize_mx(x[0], y[0], ap(in_)), rg(in_), rg(x, y))

    def act(out, in_, f, **kw):
        op("a", lambda: g.scalar.activation(ap(out), ap(in_), f, **{k: ap(kw[k]) for k in kw}), rg(in_, *kw.values()), rg(out))

    bank = [0]

    def mm(lq, ls, la, rq, rs, ra, n=128):
        b = 512 * (bank[0] % 8)
        bank[0] += 1
        l, m, r, s = V(lq, la, la + 128), V(ls, la, la + 128), V(rq, ra, ra + n), V(rs, ra, ra + n)
        op("t", lambda: g.tensor.matmul_mx(T.ps[:, b:b + n], l[0], m[0], r[0], s[0], True, True), rg(l, m, r, s), rg(V("ps", b, b + 512)))
        return b

    def PS(b, lo, hi, part=ALL):
        return (V("ps", b + lo, b + hi, part=part)[0], rg(V("ps", b, b + 512)))

    def iota(v, pattern, cm=0):
        if v[1][0][0] == "pi":
            op("g", lambda: g.iota(v[0], pattern, 0, cm), [], v[1])
        else:
            op("g", lambda: g.iota(v[0], pattern, 0, cm, allow_small_or_imprecise_dtypes=True), [], v[1])

    def do(calls):
        for c in calls:
            c[0](*c[1:])

    dma("a", "dq", (V("qb", 0, 20), T.qt[:, 0:20]))
    dma("s", "dc", (V("cb", 0, 512), T.c[:, 0:512]))
    ONE = V("onef", 0, 128)
    fill(ONE, 1.0)
    iota(V("pi", 0, 1), [[0, 1]], 1)
    op("g", lambda: g.affine_select(T.fd[:, 0:128], ONE[0], [[1, 128]], A.is_ge, PREV, 0, -1), ONE[1], rg(V("fd", 0, 128)))
    iota(V("j33", 0, 33), [[1, 33]])
    iota(V("pay", 0, 1), [[0, 1]], 1)
    iota(V("j3", 0, 32, half="all"), [[16, 2], [0, 2], [1, 16]])
    iota(V("pl", 0, 128), [[1, 128]])
    fill(V("zeros", 0, 128), 0.0)
    fill(V("ones", 0, 160), 1.0)
    fill(V("s0", 0, 256, 2), 0.0)
    fill(V("zerof", 0, 32), 0.0)
    fill(V("z8", 0, 8), 0)
    fill(V("ua", 192, 256, 2, half="all"), 0.0)
    fill(V("ua", 257, 258, half="all"), -TINY)
    ts(V("pj", 0, 1), V("pi", 0, 1), 128 - 1 - 16, A.bitwise_and)
    cp(V("f0", 0, 256, 2), V("fd", 0, 128))
    ts(V("f0", 1, 256, 2), V("fd", 0, 128), TINY, A.mult)
    for c in range(2):
        ts(V("dl", c, c + 1), V("pj", 0, 1), 16.0 * c, A.add)
    def steps(*ts):
        for t in ts:
            act(V("fn", 128 * t, 128 * t + 128), V("fd", 0, 128), F.Copy, scale=-1.0)

    steps(0, 1, 2)
    ts(V("j33", 0, 32), V("j33", 0, 32), -0.5, A.add)
    fill(V("j33", 32, 33), 31.0)

    def rep(t, on, es=range(4)):
        for e in es:
            o, q = (T.rb[:, 512 * t + e:512 * t + 512:4], [("rb%d" % e, t, t + 1, 0, 128, None)]), V("qb", 4 * t + e, 4 * t + e + 1)
            if on == "v":
                ts(o, V("ones", 0, 128), q, A.mult)
            else:
                act(o, V("zeros", 0, 128), F.Identity, bias=q)

    def quantq(t):
        quant(*(("rq", "rs", 128 * t, 128 * t + 128) if t < 4 else ("r4", "s4", 0, 128)), (T.rb[:, 512 * t:512 * t + 512], [("rb%d" % e, t, t + 1, 0, 128, None) for e in range(4)]))

    def square(dst, b, lo, hi):
        act(dst, PS(b, lo, hi), F.Square)

    def move(m, n, a, b):
        return ((AS(V("win%d" % n, a, b), dt.uint8), AS(V("win%d" % m, a, b), dt.uint8)), (V("wis%d" % n, a, b), V("wis%d" % m, a, b)))

    def row(n, t):
        return V(n, 128 * t, 128 * t + 128)

    def LIST(t, i):
        a = 512 * t + 256 * (i if t else 0) + 254
        return V("ls", a, a + 2)

    def RANK(t):
        return V("cs", 159, 160) if t else V("cs", 127, 128)

    def send(t, i, *moves):
        d = T.cores[rank ^ [1, 2, 4, 1, 2][t]]
        rid, pid = topo.addr(d, core)
        es = topo.engines(core, d)
        arr, snd = "arr" + i, "snd" + i
        if i[0] == "q":
            n = len(es) // 2
            waits("g", rg(moves[0][1], moves[1][1]), [])
            g.remote_dma_fused([RemoteDMATransfer(dst_ids=[DstId(rid=rid, pnc=pid)], dma_engine_mask=sum(1 << e for e in s), remote_sem=T.sem[arr],
                                                  srcs=[in_[0]], dsts=[out[0]]) for (out, in_), s in zip(moves, (es[:n], es[n:]))], local_sem=T.sem[snd])
            ends[snd] = ends[arr] = 2 * n
            for (out, in_) in moves:
                wr.setdefault(out[1][0][0], []).append((out[1][0], "x", arr, ends[arr]))
            return
        ends[snd] = ends[arr] = len(es) * len(moves)
        for (out, in_) in moves:
            waits("g", in_[1], [])
            g.remote_dma(out[0], in_[0], T.sem[arr], T.sem[snd], pid, rid, sum(1 << e for e in es))
            wr.setdefault(out[1][0][0], []).append((out[1][0], "x", arr, ends[arr]))

    def columns(q, s, a, qq, ss, b, n):
        return ((AS(V(q, a, a + n), dt.uint8), AS(V(qq, b, b + n), dt.uint8)), (V(s, a, a + n), V(ss, b, b + n)))

    def pick(q, s, a, qq, ss, n, off, k=32):
        act(V(s, a, a + k), IX(V(ss, 0, n), off), F.Copy)
        cp(AS(V(q, a, a + k), dt.uint32), IX(AS(V(qq, 0, n), dt.uint32), off))

    def mark(t, i):
        for c, h in ((0, LO), (32, HI)):
            ts(V("oh%d" % i, c, c + 32, part=LO, half="all"), V("j3", 0, 32, part=h, half="all"), V("cs", RANK(t)[1][0][1], RANK(t)[1][0][2], part=h),
               A.is_equal, V("pay", 0 if i else t, 1 if i else t + 1, part=h), A.mult)

    def turn(i, a=0, b=3):
        for c, to, h in ((0, LO, LO), (64, B1, B0), (64, B0, B1))[a:b]:
            tr(V("ht%d" % i, c, c + 64, part=to, half="all"), V("oh%d" % i, 0, 64, part=h, half="all"))

    def gather(t, i, h):
        a = 512 * t + 256 * i
        for j in range(2):
            scan(V("ls", a + j, a + 256, 2, part=h), V("ones", 0, 128, part=LO), V("ht%d" % i, 0, 128, part=LO, half=j), 0.0, A.max)

    def leave(t, *between):
        n = 160 if t else 128
        ts(V("cm", 0, n), V("xa", 1, 2 * n, 2), V("uc", 32, 33), A.is_gt if t else A.is_lt)
        do(between[0])
        scan(V("cs", 0, n), V("ones", 0, n), V("cm", 0, n), -32.0 if t else 0.0, A.add)
        do(between[1])
        i = 0
        mark(t, i)
        if t < 4:
            signs(t)
        do(between[2])
        if t == 3:
            newslot(t)
        turn(i)
        if t == 0:
            newslot(t)
        do(between[3])
        gather(t, i, LO)
        gather(t, i, HI)
        if t in (0, 3):
            send(t, "l%d" % t, (V("lin%d" % t, 0, 2), LIST(t, i)))
        do(between[4])
        if t in (1, 2, 4):
            hand(t)

    def hand(t):
        pick("out%d" % t, "ous%d" % t, 0, "win%d" % t, "wis%d" % t, WW[t], LIST(t, 0))
        send(t, "c%d" % t, *columns("win%d" % (t + 1), "wis%d" % (t + 1), WW[t + 1] - 32, "out%d" % t, "ous%d" % t, 0, 32))

    def slots(t):
        ts(V("pay", t, t + 1), V("nz", 0, 1), V("nz", 1, 2), A.min, V("pay", t - 1, t), A.max)

    def newslot(t):
        ts(V("nz", 0, 1), RANK(t), 128.0 + 32 * t, A.add)

    def signs(t):
        act(V("ab", 0, 33), V("j33", 0, 33), F.Abs, scale=-1.0, bias=RANK(t))
        act(V("nz", 1, 2), RANK(t), F.Relu, scale=-ROOT / 16, bias=31.5 * ROOT / 16)
        act(V("sg", 0, 33), V("ab", 0, 33), F.Sign, bias=-0.75)

    def ready(t, between=()):
        lp = LIST(t - 1, 1)
        act(V("fa", 0, 64, 2), IX(V("fn", 0, 128), lp), F.Copy)
        act(V("fa", 1, 64, 2), IX(V("fn", 0, 128), lp), F.Copy, scale=TINY)
        scatter(row("fn", t), lp, V("zerof", 0, 32))
        do(between)
        tt(V("xa", 1, 256, 2), row("km", t), row("fn", t), A.mult)

    def diag(t):
        act(V("dg", 0, 32), IX(row("km", t), V("dl", 0, 2)), F.Copy)

    def turned():
        tr(V("dc", 0, 32), V("dg", 0, 32))

    def start():
        ts(V("col", 2, 3), V("nz", 1, 2), -ROOT, A.mult, V("dc", 0, 1), A.subtract)

    def own(t):
        square(row("sq", t), mm("rq", "rs", 128 * t, "win0", "wis0", 0), 0, 128)

    def uses(t, a, b):
        c = 128 * t
        tt(V("kk", c + a, c + b), V("kk", c - 128 + a, c - 128 + b) if t > 1 else V("s0", 2 * a + 1, 2 * b, 2), V("sq", c + a, c + b), A.add)

    def floor(t):
        ts(row("km", t), row("kk", t), TINY, A.max)

    def UA(t, a, b):
        o = 128 - 32 * t
        return V("ua", 2 * (o + a) + 1, 2 * (o + b), 2, half=t - 1)

    def YB(t, o):
        return V("yy", 256 * t + 128 * o, 256 * t + 128 * o + 128)

    def under_w(t, os=range(O)):
        for o in os:
            a, n = (0, 192) if t == 2 else (128, 128)
            b = mm("wq", "ws", 128 * o, "win%d" % t, "wis%d" % t, a, n)
            act(V("zl", 128 * o + 32 * t - 64, 128 * o + 32 * t), PS(b, n - 64, n), F.Copy)
            if t == 2:
                act(YB(0, o), PS(b, 0, 128), F.Copy)

    def UF(t, a, b):
        return V("uf", 96 * (t % 2) + a, 96 * (t % 2) + b)

    def SN(t, a, b):
        return V("sn", 96 * (t % 2) + a, 96 * (t % 2) + b)

    def more(t, a, b):
        tt(UA(t, a, b), UA(t - 1, a, b), SN(t, a, b), A.add)

    def raised(t, a, b):
        ts(UF(t, a, b), UA(t, a, b), TINY, A.max)

    def spread(j):
        act(V("nc", 32 * j, 32 * j + 32), V("zerof", 0, 32), F.Identity, bias=V("ni3", j, j + 1))

    def lay(t, o):
        scatter(YB(t, o), LIST(t, 1), V("zl", 128 * o + 32 * t, 128 * o + 32 * t + 32))

    def keep(t, o):
        act(YB(t + 1, o), YB(t, o), F.Copy)
        if o == 1:
            dma("s", "dy%d" % t, (T.y[:, 256 * t:256 * t + 256], V("yy", 256 * t, 256 * t + 256)))

    def older(t, s):
        scatter(row("km", t), LIST(s, 1), UF(t, 32 * s, 32 * s + 32))

    def landed(t):
        w = ("win%d" % t, "wis%d" % t, 32 * t)
        if t == 1:
            cp(UA(1, 0, 32), IX(V("sp", 0, 128), V("lin0", 0, 2)))
            act(SN(2, 0, 32), IX(V("sp", 128, 256), V("lin0", 0, 2)), F.Copy)
            pick("win1", "wis1", 128, "pre", "prs", 128, V("lin0", 0, 2))
        elif t == 2:
            square(UA(2, 32, 64), mm("rq", "rs", 256, *w), 96, 128)
            square(SN(3, 0, 64), mm("rq", "rs", 384, *w), 64, 128)
            b = mm("r4", "s4", 0, "win2", "wis2", 0, 192)
            square(row("sq", 4), b, 0, 128)
            square(SN(4, 0, 64), b, 128, 192)
            under_w(2)
        elif t == 3:
            square(UA(3, 64, 96), mm("rq", "rs", 384, *w), 96, 128)
            square(SN(4, 64, 96), mm("r4", "s4", 0, *w), 96, 128)
            square(V("nb", 0, 64), mm("xq", "xs", 0, *w), 64, 128)
        scan(V("uc", 0, 33), V("sg", 0, 33), V("ua", 193, 258, 2, half=t - 1), V("col", 2, 3), A.min)
        scan(V("xa", 256, 320), V("ua", 192, 256, half=t - 1), V("fa", 0, 64), 0.0, A.min)
        if t == 1:
            wait("s", "arrl0", ends["arrl0"])
            dma("s", "dn2", *move(0, 2, 0, 128))
        if t < 4:
            dma("s", "dg%d" % (t + 1), *move(t, t + 1, 128, 128 + 32 * t))
            dma("s", "dn%d" % (t + 2), *move(0, t + 2, 0 if t < 3 else 32, 128))

    def query(q, s, b, qq, ss, a):
        return (AS(V(q, b, b + 2), dt.uint8), AS(V(qq, a, a + 2), dt.uint8)), (V(s, b, b + 8), V(ss, a, a + 8))

    rep(0, "v")
    quant("win0", "wis0", 0, 128, V("cb", 0, 512))
    quantq(0)
    send(0, "c0", *columns("pre", "prs", 0, "win0", "wis0", 0, 128))
    rep(1, "a")
    rep(4, "a", (0, 1))
    square(V("s0", 1, 256, 2), mm("rq", "rs", 0, "win0", "wis0", 0), 0, 128)
    b = mm("win0", "wis0", 0, "rq", "rs", 0)
    dma("s", "dn1", *move(0, 1, 0, 128))
    dma("s", "dw", (V("wb", 0, 1024), T.w[:, 0:1024]))
    rep(2, "v")
    quantq(1)
    own(1)
    quantq(2)
    own(2)
    rep(4, "a", (2, 3))
    rep(3, "v")
    ts(V("uc", 32, 33), PS(b, 0, 1), PS(b, 0, 1), A.mult, TINY, A.max)
    scan(V("xa", 0, 256), V("s0", 0, 256), V("f0", 0, 256), 0.0, A.max)
    quantq(3)
    leave(0, [(uses, 1, 0, 64)], [(uses, 1, 64, 128)], [(quantq, 4)], [(floor, 1), (diag, 1)],
          [(slots, 1), (turned,)])
    send(3, "q4", *query("pq", "pqs", 0, "r4", "s4", 0))
    for q in (1, 2):
        square(V("sp", 128 * q - 128, 128 * q), mm("rq", "rs", 128 * q, "pre", "prs", 0), 0, 128)
    ready(1, [(start,), (uses, 2, 0, 64)])
    def second(t, *more_calls):
        return [(mark, t, 1)], [(turn, 1)], [(gather, t, 1, LO)] + list(more_calls)

    def BLOCK(d):
        return (32 * d, 32 * d + 32)

    def quantw(o):
        quant("wq", "ws", 128 * o, 128 * o + 128, V("wb", 512 * o, 512 * o + 512))

    def where(t):
        act(V("pl", 128 + 32 * t, 160 + 32 * t), IX(V("pl", 0, 128 + 32 * t), LIST(t, 0)), F.Copy)

    def twice(t):
        for j in range(2):
            act(V("dd", 0, 32, half=j), IX(V("pl", 0, 128 + 32 * t), LIST(t, 0)), F.Copy)

    def across():
        for c in range(2):
            tr(V("dt", 32 * c, 32 * c + 32), V("dd", 16 * c, 16 * c + 16, half="all"))

    def listed(t):
        cp(LIST(t, 1), V("dt", 0, 64, 32))

    landed(1)
    where(0)
    own(3)
    square(V("sx", 0, 128), mm("r4", "s4", 0, "pre", "prs", 0), 0, 128)
    steps(3, 4)
    uses(2, 64, 128)
    leave(1, [(more, 2, 0, 32)], [(floor, 2), (raised, 2, 0, 32)], [(uses, 3, 0, 64)], [(older, 2, 0), (diag, 2)], [(newslot, 1)])
    twice(1)
    where(1)
    turned()
    uses(3, 64, 128)
    slots(2)
    start()
    across()
    floor(3)
    listed(1)
    quantw(0)
    ready(2, [(quantw, 1)])
    pick("xq", "xs", 0, "pq", "pqs", 2, V("z8", 0, 8), 128)

    landed(2)
    leave(2, [(more, 3, 0, 64)], [(raised, 3, 0, 64), (uses, 4, 0, 64)], [(uses, 4, 64, 128)], [(older, 3, 0)], [(newslot, 2)])
    older(3, 1)
    twice(2)
    diag(3)
    where(2)
    more(4, 0, 64)
    across()
    floor(4)
    slots(3)
    listed(2)
    raised(4, 0, 64)
    turned()
    ready(3, [(older, 4, 0), (start,)])
    older(4, 1)
    act(V("sx", 128, 160), IX(row("sq", 4), LIST(0, 0)), F.Copy)
    lay(0, 0)

    landed(3)
    more(4, 64, 96)
    a, b, c = second(3, (gather, 3, 1, HI))
    leave(3, [(raised, 4, 64, 96), (tr, V("nt", 0, 64, 2), V("nb", 0, 32)), (tr, V("nt", 1, 64, 2), V("nb", 32, 64)),
              (send, 3, "n3", (V("ni3", 0, 2), V("nt", 0, 2)))], [(older, 4, 2)], a + [(diag, 4), (spread, 0), (spread, 1)], b, c + [(turned,)])
    hand(3)
    ready(4, [(start,), (slots, 4), (tr, V("sx", 160, 224), V("nc", 0, 64))])
    cp(UA(4, 96, 128), IX(V("sx", 0, 224), V("lin3", 0, 2)))

    keep(0, 0)
    where(3)
    landed(4)
    lay(0, 1)
    keep(0, 1)
    leave(4, [(lay, 1, 0), (keep, 1, 0)], [], [], [(lay, 1, 1), (keep, 1, 1)], [])
    under_w(4)
    lay(2, 0)
    keep(2, 0)
    lay(2, 1)
    keep(2, 1)
    twice(4)
    lay(3, 0)
    keep(3, 0)
    lay(3, 1)
    wait("s", "sndc4", ends["sndc4"])
    keep(3, 1)
    across()
    listed(4)

    bs = [mm("wq", "ws", 128 * o, "win5", "wis5", 32) for o in range(O)]
    for o in range(O):
        cp(V("zf", 32 * o, 32 * o + 32), PS(bs[o], 96, 128))
    for o in range(O):
        scatter(YB(4, o), LIST(4, 1), V("zf", 32 * o, 32 * o + 32))
        dma("s" if o == 0 else "a", "dy%d" % (4 + o), (T.y[:, 1024 + 128 * o:1152 + 128 * o], YB(4, o)))
    for s in sorted(ends):
        if s not in ("dy4", "dy5"):
            wait("g", s, ends[s])
    for q in ("g", "t", "a", "v"):
        wait("g", csem[q], count[q])
    wait("s", "dy4", ends["dy4"])
    wait("a", "dy5", ends["dy5"])
